import numpy as np, ml_dtypes
CORES = [13,21,141,149]
N = 4
BF = ml_dtypes.bfloat16
M, L, S, E, G0, T, Q, W = 1744, 192, 64, 4, 2, 4, 560, 1952
LV = [235, 436, 604, 405]
def forest(rng, lean):
    sn = np.full((16, M), M); fa = rng.integers(0, M, M); gn = np.zeros(M, np.int64)
    o = 64 + rng.permutation(M - 64); cur = np.arange(64); at = 0
    for i, n in enumerate(LV):
        nxt = o[at:at + n]; at += n
        share = 0.9 if i == 0 else 0.45 + 0.3 * rng.random()
        fert = rng.permutation(cur)[:max(n // 16 + 1, int(len(cur) * share))]
        key = rng.random((len(fert), 16)) * np.exp2(lean * rng.random((len(fert), 1)))
        pk = np.argsort(key.reshape(-1))[:n]; dad = fert[pk >> 4]
        sn[pk & 15, dad] = nxt; fa[nxt] = dad; gn[nxt] = i + 1; cur = nxt
    return sn, fa, gn
def woods(rng, lean):
    v = [forest(rng, lean) for _ in range(8 * N)]
    return np.stack([a[0] for a in v]).reshape(N, 8, 16, M), np.stack([a[1] for a in v]).reshape(N, 8, M), np.stack([a[2] for a in v]).reshape(N, 8, M)
def pack(x, w, sn, fa, gn):
    return {"x": np.ascontiguousarray(x.reshape(N, 128, M)).astype(np.float32).astype(BF), "w": np.ascontiguousarray(w.reshape(N, 128, 1)).astype(np.float32).astype(BF),
            "sn": np.ascontiguousarray(sn.reshape(N, 128, M)).astype(np.int32), "fa": fa.astype(np.int32), "gn": gn.astype(np.int32)}
def few(rng, sn, fa, gn, n):
    if n: sn[:, 64] = M; sn[:, M - 1] = M
    z = int(rng.integers(0, 64)); sn[:, z] = M
    empty = np.all(sn == M, axis=0); gn[empty] = np.minimum(gn[empty], G0 - 1)
    if n:
        o = np.flatnonzero(empty); o = rng.permutation(o[(o > 64) & (o < M - 1)])[:n - 2]
        o = np.concatenate([np.array([64, M - 1]), o]); fa[o] = z; gn[o] = G0 + rng.integers(0, 2, len(o))
def ladders(rng, sn, fa, gn):
    U = (E - 2) // 2 + 1; B = 2 * U + 4; nb = (M - 64) // B
    sn[:] = M; gn[:] = 0; fa[:] = rng.integers(0, 64, M)
    k = (64 + rng.permutation(M - 64))[:nb * B].reshape(nb, B); u = rng.integers(0, U + 1, nb); a = rng.integers(0, 16, nb)
    for j in range(U + 1):
        m = j <= u; up = k[m, j]; so = k[m, 1 + j]
        sn[a[m] if j == 0 else rng.integers(0, 16, len(up)), up] = so; fa[so] = up
    a = (a + 1 + rng.integers(0, 15, nb)) & 15
    for j in range(U + 2):
        m = j <= u + 1; up = k[m, 0 if j == 0 else U + 1 + j]; so = k[m, U + 2 + j]
        sn[a[m] if j == 0 else rng.integers(0, 16, len(up)), up] = so; fa[so] = up
    gn[k[np.arange(nb), 1 + u]] = G0 + rng.integers(0, 2, nb)
    sn[:4, :64] = rng.choice(k[:, 0], (4, 64))
def guests(rng, x, sn, fa, gn):
    n = S - int(rng.integers(0, 4)); z = int(rng.integers(1, 64)); o = 64 + rng.permutation(M - 64)
    last = M - 16 - np.arange(n); o = np.concatenate([last, o[~np.isin(o, last)]])
    s, p, q, y, h, r, u, v = o[:8 * n].reshape(8, n); h = np.sort(h)
    x[:] = rng.integers(0, 256, (16, M)); sn[:] = M; fa[:] = rng.integers(0, M, M); gn[:] = rng.integers(0, G0, M)
    deck = [np.arange(64)] + np.array_split(o[8 * n:], E)
    for a, b in zip(deck[:-1], deck[1:]):
        m = rng.random((16, len(a))) < 0.3; m[rng.integers(0, 16, len(a)), np.arange(len(a))] = True
        sn[:, a] = np.where(m, rng.choice(b, (16, len(a))), M); fa[b] = rng.choice(a, len(b))
    sn[:, z] = M
    for top, one, two in ((p, q, y), (y, h, r), (r, s, u)):
        i = rng.integers(0, 16, n); j = (i + rng.integers(1, 16, n)) & 15
        sn[i, top] = one; sn[j, top] = two; fa[one] = top; fa[two] = top
    sn[rng.integers(0, 16, n), s] = v; fa[v] = s; fa[h] = z; gn[q] = G0; gn[h] = G0
    x[:, h] = x[:, q]; x[:, r] = 255 - x[:, q]; x[:, u] = 255 - x[:, q]
    x[:, s] = x[:, q]; x[:8, s] = x[:8, s] ^ rng.integers(0, 2, (8, n))
def doubles(rng, o, x, sn, fa, gn, nought):
    n = len(o) // 8; p, g, y, z, v, u, a, b = o[:8 * n].reshape(8, n)
    h = 1 + rng.permutation(31)[:n]
    if nought: h[0] = 0
    sn[:, o] = M; sn[:, h] = M; fa[h] = p; fa[p] = g; gn[h] = G0
    up = np.arange(n) % 2 == 1; top = np.where(up, g, p); low = np.where(up, p, h); k = np.argsort(rng.random((n, 16)), axis=1).T
    sn[k[0], top] = low; sn[k[1], top] = low; sn[np.minimum(k[2], k[3]), top] = z; sn[np.maximum(k[2], k[3]), top] = y
    sn[k[4][up], p[up]] = h[up]; sn[k[5][up], p[up]] = h[up]
    sn[k[6], y] = v; sn[k[7], z] = u; sn[k[8], v] = a; sn[k[9], u] = b
    end = 255 * rng.integers(0, 2, (16, n)); m = rng.integers(0, 64, (16, n)) * ((np.arange(n) // 2) % 2)
    one = np.zeros((16, n), np.int64); one[rng.integers(0, 16, n), np.arange(n)] = 1
    x[:, h] = end; x[:, p] = end; x[:, z] = np.abs(255 - end - m); x[:, y] = np.abs(255 - end - m - one)
    return h
def setup_inputs(rng):
    sn, fa, gn = woods(rng, 3.0)
    return pack(rng.integers(0, 256, (N, 8, 16, M)), rng.integers(0, 16, (N, 8, 16, 1)), sn, fa, gn)
def setup_inputs_again(rng):
    sn, fa, gn = woods(rng, 2.0); base = rng.choice(np.array([0, 7, 130, 254]), (N, 8, 1, 1))
    x = base + np.where(rng.random((N, 8, 1, M)) < 0.75, rng.integers(0, 2, (N, 8, 1, M)), rng.integers(0, 2, (N, 8, 16, M)))
    for g in rng.permutation(8)[:4]:
        for q in range(N): guests(rng, x[q, g], sn[q, g], fa[q, g], gn[q, g])
    return pack(x, rng.integers(0, 16, (N, 8, 16, 1)), sn, fa, gn)
def setup_inputs_corners(rng):
    sn, fa, gn = woods(rng, 3.0)
    for q in range(N):
        for g, kind in enumerate(rng.permutation(8)):
            s, f_, n_ = sn[q, g], fa[q, g], gn[q, g]
            if kind < 6: few(rng, s, f_, n_, (S, S + 1, S - 1, L, L + 1, 0)[int(kind)])
            elif kind == 6:
                half = rng.permutation(M)[:M // 2]; s[:] = M; s[:, half] = rng.integers(0, M, (16, len(half)))
                f_[:] = rng.choice(half, M); n_[:] = rng.integers(0, E + 1, M)
            else: ladders(rng, s, f_, n_)
    return pack(rng.integers(0, 256, (N, 8, 16, M)), rng.integers(0, 16, (N, 8, 16, 1)), sn, fa, gn)
def setup_inputs_ends(rng):
    w = 15 * rng.integers(0, 2, (N, 8, 16, 1))
    for q in range(N):
        full, none = rng.permutation(8)[:2]
        if q == N - 1: full, none = 7, 0
        w[q, full] = 15; w[q, none] = 0
    x = 255 * np.where(rng.random((N, 8, 1, M)) < 0.6, rng.integers(0, 2, (N, 8, 1, M)), rng.integers(0, 2, (N, 8, 16, M))); x[..., 0] = 0; x[..., M - 1] = 255
    gn = E * rng.integers(0, 2, (N, 8, M)); sn = np.full((N, 8, 16, M), M)
    fa = np.where(rng.random((N, 8, M)) < 0.68, (M - 1) * rng.integers(0, 2, (N, 8, M)), rng.integers(0, M, (N, 8, M)))
    for q in range(N):
        for g in range(8):
            fer = rng.random(M) < 0.45; fer[:64] = True; fer[M - 1] = g % 2 == 0; fc = np.flatnonzero(fer)
            u = rng.random(M); m = rng.random((16, M)) < 0.3; m[:, u < 0.25] = False; m[15, u < 0.25] = True; m[:, u > 0.9] = True
            v = np.where(rng.random((16, M)) < 0.75, rng.choice(fc, (16, M)), rng.integers(0, M, (16, M)))
            v = np.where(rng.random((16, M)) < 0.12, (M - 1) * rng.integers(0, 2, (16, M)), v)
            sn[q, g] = np.where(m & fer, v, M); sn[q, g, 15, 0] = 0
            if g % 2 == 0:
                far = fc[np.all(x[q, g][:, fc] == 255, axis=0)]; sn[q, g, :, M - 1] = rng.choice(far, 16)
            else: gn[q, g, M - 1] = E; fa[q, g, M - 1] = rng.choice(fc)
    return pack(x, w, sn, fa, gn)
def setup_inputs_loops(rng):
    fa = rng.integers(0, M, (N, 8, M)); fa = np.where(rng.random((N, 8, M)) < 0.05, np.arange(M), fa)
    gn = rng.integers(0, E + 1, (N, 8, M)); sn = np.full((N, 8, 16, M), M); x = rng.integers(0, 256, (N, 8, 16, M))
    for q in range(N):
        for g in range(8):
            m = rng.random((16, M)) < rng.choice(np.array([0.0, 0.0, 0.06, 0.4, 1.0]), M)
            v = rng.integers(0, M, (16, M))
            if g % 2: v = rng.choice(rng.permutation(M)[:200], (16, M))
            v = np.where(rng.random((16, M)) < 0.03, np.arange(M), v); s = np.where(m, v, M)
            far = 64 + rng.permutation(M - 64); o = far[:192]; a, b, h = o[:64], o[64:128], o[128:]
            s[:, o] = M; s[5, a] = b; s[9, b] = h; s[11, b[:20]] = h[:20]; fa[q, g, h] = a; gn[q, g, h] = G0
            e = doubles(rng, far[192:384], x[q, g], s, fa[q, g], gn[q, g], g % 2 == 0)
            if g % 2:
                s[:, 32:64] = M; s[3, 32:64] = rng.choice(a, 32); s[:, 0] = M; fa[q, g, 0] = e[0]; gn[q, g, 0] = G0
            sn[q, g] = s
    return pack(x, rng.integers(0, 16, (N, 8, 16, 1)), sn, fa, gn)
def setup_inputs_spread(rng):
    sn, fa, gn = woods(rng, 9.0)
    x = (rng.random((N, 8, 16, M)) * np.exp2(8 * rng.random((N, 8, 1, M))) * (rng.random((N, 8, 1, M)) > 0.0625)).astype(np.int64)
    w = (rng.random((N, 8, 16, 1)) * np.exp2(4 * rng.random((N, 8, 16, 1)))).astype(np.int64)
    return pack(np.minimum(x, 255), np.minimum(w, 15), sn, fa, gn)
def check_inputs(d):
    bad = []
    for k, lo, hi in (("x", 0, 255), ("w", 0, 15), ("sn", 0, M), ("fa", 0, M - 1), ("gn", 0, E)):
        v = np.asarray(d[k]).astype(np.float64)
        if not (np.min(v) >= lo and np.max(v) <= hi): bad.append("range of " + k)
        elif np.any(v != np.floor(v)): bad.append("whole numbers in " + k)
    return bad
def narrow(tab, ix):
    return np.take_along_axis(tab, ix, 2)
def broad(tab, ix):
    return np.take_along_axis(tab, ix[:, :, None, :], 3)
def reference(x, w, sn, fa, gn):
    X = np.zeros((N, 8, 16, W), np.int32); X[..., :M] = x.astype(np.float32).reshape(N, 8, 16, M)
    SN = np.full((N, 8, 16, W), M, np.int64); SN[..., :M] = sn.reshape(N, 8, 16, M)
    F1 = np.zeros((N, 8, W), np.int64); F1[..., :M] = fa; F2 = F1.copy()
    GN = np.zeros((N, 8, W), np.int64); GN[..., :M] = gn
    wt = w.astype(np.float32).astype(np.int32).reshape(N, 8, 16, 1)
    ship_x = np.zeros((N, 8, 16, S), np.int32); ship_d = np.zeros((N, 8, S), np.int64); ship_h = np.full((N, 8, S), M)
    own = np.arange(L + S) < L; lower = np.tri(L, k=-1).astype(bool)
    for t in range(T):
        f = (F1 if t % 2 == 0 else F2).copy()
        order = (np.arange(W) + t * Q) % W
        ok = (np.all(SN == M, axis=2) & (GN >= G0))[..., order]; place = np.add.accumulate(ok.astype(np.int64), axis=2) - ok
        i, j, k = np.nonzero(ok & (place < L)); h = np.full((N, 8, L), M); h[i, j, place[i, j, k]] = order[k]
        xh = broad(X, h); ax = np.roll(ship_x, t, axis=0)
        xl = np.concatenate([xh, ax], axis=3); real = h != M
        live = np.concatenate([real, np.roll(ship_h, t, axis=0) != M], axis=2)
        c = np.concatenate([narrow(f, h), np.add.reduce(wt * ax, axis=2).astype(np.int64) & 63], axis=2); p = c.copy()
        b = np.concatenate([h, np.full((N, 8, S), M)], axis=2); up_n = np.ones((N, 8, L + S), np.int64)
        d = np.concatenate([np.full((N, 8, L), 2), np.roll(ship_d, t, axis=0)], axis=2)
        y = np.full((N, 8, L + S), M); s = y.copy(); a = np.zeros((N, 8, L + S), np.int64); found = np.zeros((N, 8, L + S), bool)
        for e in range(E):
            sons = broad(SN, c)
            can = (sons != M) & (sons != b[:, :, None, :])
            xs = broad(X, np.ascontiguousarray(sons.transpose(0, 1, 3, 2)).reshape(N, 8, -1)).reshape(N, 8, 16, L + S, 16)
            score = np.add.reduce(np.abs(xs - xl[..., None]), axis=2)
            best = np.argmin(np.where(can.transpose(0, 1, 3, 2), score, 2 ** 20), axis=3)
            son = np.take_along_axis(sons, best[:, :, None, :], 2)[:, :, 0]; some = np.any(can, axis=2)
            down = live & some; fail = live & ~some & (~own | (p < 64)); up = live & ~some & ~fail
            y = np.where(down, c, y); s = np.where(down, son, s); a = np.where(down, best, a); d = np.where(down, d - 1, d)
            hit = down & (d == 0); found = found | hit; live = live & ~fail & ~hit
            fp = narrow(f, p); up_n = np.where(up, up_n + 1, up_n); d = np.where(up, up_n + 1, d)
            b = np.where(up, p, np.where(down, M, b)); c = np.where(up, fp, np.where(down, son, c)); p = np.where(up, fp, p)
        fo, yo, so, ao = found[..., :L], y[..., :L], s[..., :L], a[..., :L]
        same = (yo[..., :, None] == yo[..., None, :]) | (so[..., :, None] == so[..., None, :])
        go = fo & ~np.any(same & fo[..., None, :] & lower, axis=3)
        several = np.add.reduce((broad(SN, yo) != M).astype(np.int64), axis=2) > 1
        mixed = (broad(X, so) + xh) >> 1
        back_x = np.roll(broad(X, s[..., L:]), -t, axis=0); back = np.roll(found[..., L:], -t, axis=0)
        lost = real & ~fo; place = np.add.accumulate(lost.astype(np.int64), axis=2) - lost; age = narrow(GN, h)
        i, j, k = np.nonzero(go); hh, yy, ss, aa = h[i, j, k], yo[i, j, k], so[i, j, k], ao[i, j, k]; m = several[i, j, k]
        SN[i, j, 0, hh] = ss; F2[i, j, ss] = hh; X[i, j, :, ss] = mixed[i, j, :, k]
        SN[i[m], j[m], aa[m], yy[m]] = M; F1[i[m], j[m], ss[m]] = hh[m]
        i, j, k = np.nonzero(back); hh = ship_h[i, j, k]; nc = M + 16 + S * (t - 1) + k
        X[i, j, :, nc] = back_x[i, j, :, k]; F1[i, j, nc] = hh; F2[i, j, nc] = hh; GN[i, j, nc] = GN[i, j, hh] + 1; SN[i, j, t, hh] = nc
        i, j, k = np.nonzero(lost & (place < S)); pl = place[i, j, k]
        ship_x = np.zeros((N, 8, 16, S), np.int32); ship_d = np.zeros((N, 8, S), np.int64); ship_h = np.full((N, 8, S), M)
        ship_x[i, j, :, pl] = xh[i, j, :, k]; ship_d[i, j, pl] = age[i, j, k]; ship_h[i, j, pl] = h[i, j, k]
    return {"xo": X.reshape(N, 128, W).astype(np.float32).astype(BF), "fo": F1.astype(np.float32), "f2o": F2.astype(np.float32)}

@@ -1,0 +1,765 @@
+from concourse.mybir import AluOpType as OP, ActivationFunctionType as AF
+
+M, W, L, S, T_, Q = 1744, 1952, 192, 64, 4, 560
+BK = 2176
+WT = BK + W
+TB = W
+HWN = W + L
+BIG = 512.0
+SW_ = 68
+NENG = 8
+
+SCRATCH = {}
+PLACE = {}
+HALF = set()
+BANKS = set("k%d" % i for i in range(8))
+POOL = {"float32": ["poolf", 0], "bfloat16": ["poolh", 0], "int32": ["pooli", 0], "uint16": ["poolu", 0]}
+
+
+def _b(kind, dtype, **kw):
+    for n, w in kw.items():
+        if dtype in ("bfloat16", "uint16"):
+            HALF.add(n)
+        if kind == "psum" or n[:2] in ("ms", "bs", "ls", "mr", "br", "lr"):
+            SCRATCH[n] = (kind, [128, w], dtype)
+        else:
+            p = POOL[dtype]
+            PLACE[n] = (p[0], p[1], w)
+            p[1] += (w + 15) // 16 * 16
+            SCRATCH[p[0]] = (kind, [128, p[1]], dtype)
+
+
+_b("sbuf", "float32", SN=WT, F1=W + L, F2=W + L, GH=W, HWIN=HWN, D=W, H=L, TMP=L, RW=L, P0=L, P1=L, S0=L, S1=L, W0=L,
+   WD=L, SA=L, HG=L, RMOD=384, DIAG=L, LTM=384, RS0=384, RST=96, D15=L, OF=128, I3=384, SW=512, ONESF=128,
+   R16=1, PBF=2, R122=1, M0=1, E0=1, TRL=12, TR4=48, POS=122, COLC=64, ZER=122, GTH=488, NOK=122, C1=122,
+   HW12=12, P0W=12, U2=24, ND=12, WALL=36, KALL=24, D1=24, YS=24, KF=12, AW=12, FND=24, YT=24, BS0=384, SCB=384,
+   DX=384, BSA=L, FR=L, FRS=L, SR=L, SRS=L, FL4=48, Z4=48, Z5=48, SY=L, DD=L, VH=L, VY=L, XG=L, LOF=12,
+   CS=12, DA=12, DB=12, RT=S, RTS=S, RTB=S, RTSB=S, FDW=4, RZ=4, RV=S, RV2=S, RVB=S, RV2B=S, FD=S, GENM=12, LB3=12, LBT=12,
+   LF=128, LG=128, G2K=128, FGF=M, MTC=8, MKEEP=384)
+for _n in ("A1", "A2", "AB"):
+    _w = 64 if _n == "AB" else 96
+    _b("sbuf", "float32", **{"SF" + _n: _w, "MM" + _n: _w, "IM" + _n: _w, "NI" + _n: _w, "ZZ" + _n: _w, "RR" + _n: _w})
+_b("sbuf", "bfloat16", X=WT, ANE=W, SEL=2048, WSEL=2048, ONES=128, ONESB=128, TRI=128, TRMO=128, SLR=128, XL=L, XR=3072,
+   XRB=1024, UA=3072, UB=1024, EQ0=L, EM0=L, EQ1=L, NINC=122, EDM=384, EE=2112, EMY=L, AX=L, LO=12, WC=1, TMPB=128,
+   FGB=M, LGB=128, VH8=W, VL8=W)
+_b("sbuf", "int32", SNI=M, FGI=M, GTI=488, PI=1, PI2=1, PAD=208, LKI=64, KI=12, KI2=12, HI4=4, HI4B=4, HIR=S, HIR2=S,
+   CI=4, CI2=4, XI=L)
+_b("sbuf", "uint16", OFF16=122, H16=L, HL=12, P0L=12, P1L=12, SA16=L, S16B=64, S16A=L, LA=12, LB=12, LK=64, BL=4,
+   YR16=384, YL=12, SL=12, L4=48, LO16=12, RL16=4, BF16=4)
+_b("psum", "float32", k0=512, k1=512, k2=512, k3=512, k4=512, k5=512, k6=512, k7=512)
+SCRATCH["gnd"] = ("dram", [8, Q * 3 + W], "int32")
+for _t in range(3):
+    _b("sbuf", "bfloat16", **{"ms%d" % _t: 384, "bs%d" % _t: SW_, "ls%d" % _t: SW_, "mr%d" % (_t + 1): S, "br%d" % (_t + 1): S, "lr%d" % (_t + 1): S})
+    _b("sbuf", "float32", **{"HGS%d" % _t: 384, "HROW%d" % _t: S, "GHN%d" % _t: S, "HSW%d" % _t: 4})
+    _b("sbuf", "uint16", **{"HS%d" % _t: 4})
+
+MSGS = [("s", 0), ("r", 1), ("s", 1), ("r", 2), ("s", 2), ("r", 3)]
+SEMAPHORES = ["qv", "qs", "qt", "qg", "lo"] + ["d%d" % i for i in range(24)] + ["x%s%d" % m for m in MSGS] + ["a%s%d" % m for m in MSGS]
+
+
+def goal(T, rank, kind, t):
+    return T.cores[(rank + 1 + t) % 4] if kind == "s" else T.cores[(rank - t) % 4]
+
+
+def via(topo, src, dst):
+    if topo.may_write(src, dst):
+        return None
+    c = [k for k in topo.cores_of(src) if k != src and topo.may_write(k, dst)]
+    near = [k for k in c if topo.die(k) == topo.die(src)]
+    return (near + c)[0]
+
+
+def send(g, topo, src, dst, out, in_, rsem, lsem):
+    rid, pid = topo.addr(dst, src)
+    mask = sum(1 << e for e in topo.engines(src, dst)[:NENG])
+    g.remote_dma(out, in_, rsem, lsem, pid, rid, mask)
+
+
+def hand_on(g, core, T, topo):
+    n = 0
+    for kind, t in MSGS:
+        for r in range(len(T.cores)):
+            dst = goal(T, r, kind, t)
+            if via(topo, T.cores[r], dst) == core:
+                k = "%s%d" % (kind, t)
+                g.wait_ge(T.sem["x" + k], NENG)
+                send(g, topo, core, dst, T["l" + k][:], T["b" + k][:], T.sem["a" + k], T.sem.lo)
+                n += NENG
+    if n:
+        g.wait_ge(T.sem.lo, n)
+
+
+def rank_program(g, core, T, topo):
+    rank = T.rank_of(core)
+    if rank is None:
+        hand_on(g, core, T, topo)
+        return
+
+    queue = {"v": g.vector, "s": g.scalar, "t": g.tensor, "g": g, "y": g.sync}
+    count = {"qv": 0, "qs": 0, "qt": 0, "qg": 0}
+    known = {e: {} for e in queue}
+    clock = {}
+    wr, rd = {}, {}
+    dsem = [0]
+    total = {}
+    WAKE, CY = 0.1, 0.00083
+    free = {e: 0.0 for e in queue}
+    when = {}
+    tape = [None]
+
+    def deps(e, reads, writes):
+        w = {}
+
+        def want(sem, val):
+            if known[e].get(sem, 0) < val and w.get(sem, 0) < val:
+                w[sem] = val
+        for isw, lst in ((0, reads), (1, writes)):
+            for n, lo, hi in lst:
+                ps = n in BANKS
+                for lo2, hi2, e2, sem, val in wr.get(n, ()):
+                    if ps and e2 != e or lo < hi2 and lo2 < hi:
+                        if not (e == "t" and e2 == "t" and ps):
+                            want(sem, val)
+                if isw or ps:
+                    for (e2, lo2, hi2), (sem, val) in rd.get(n, {}).items():
+                        if ps and e2 != e or (isw and lo < hi2 and lo2 < hi):
+                            want(sem, val)
+        return w
+
+    def need(e, reads, writes):
+        w = deps(e, reads, writes)
+        for sem in w:
+            free[e] = max(free[e], when.get((sem, w[sem]), 0) + WAKE)
+        for sem in sorted(w):
+            if known[e].get(sem, 0) >= w[sem]:
+                continue
+            queue[e].wait_ge(T.sem[sem], w[sem])
+            known[e][sem] = w[sem]
+            for s2, v2 in clock.get((sem, w[sem]), {}).items():
+                if known[e].get(s2, 0) < v2:
+                    known[e][s2] = v2
+
+    def note(e, sem, val, reads, writes):
+        c = dict(known[e])
+        if sem[0] == "q":
+            for s2, v2 in clock.get((sem, val - 1), {}).items():
+                if c.get(s2, 0) < v2:
+                    c[s2] = v2
+        c[sem] = val
+        clock[(sem, val)] = c
+        total[sem] = max(total.get(sem, 0), val)
+        for n, lo, hi in writes:
+            wr[n] = [x for x in wr.get(n, []) if not (lo <= x[0] and x[1] <= hi)] + [(lo, hi, e, sem, val)]
+            rd[n] = {k: x for k, x in rd.get(n, {}).items() if not (lo <= k[1] and k[2] <= hi)}
+        for n, lo, hi in reads:
+            rd.setdefault(n, {})[(e, lo, hi)] = (sem, val)
+
+    def flat(xs):
+        r = []
+        for x in xs:
+            if x is not None and not isinstance(x, (int, float)):
+                r += [x[0:3]] if len(x) == 4 else [x[0][0:3], x[1][0:3]]
+        return r
+
+    def ap(x):
+        return x if x is None or isinstance(x, (int, float)) else x[3] if len(x) == 4 else x[2]
+
+    def emit(e, call, reads, writes, us):
+        if tape[0] is not None:
+            tape[0].append((e, call, flat(reads), flat(writes), us))
+        else:
+            issue(e, call, flat(reads), flat(writes), us)
+
+    def issue(e, call, reads, writes, us):
+        need(e, reads, writes)
+        free[e] += us
+        if writes:
+            sem = "q" + e
+            count[sem] += 1
+            call().then_inc(T.sem[sem], 1)
+            when[(sem, count[sem])] = free[e]
+            note(e, sem, count[sem], reads, writes)
+        else:
+            call()
+
+    def record(gen):
+        tape[0] = []
+        for _ in gen:
+            pass
+        r = tape[0]
+        tape[0] = None
+        return r
+
+    def merge(streams):
+        pos = {n: 0 for n in streams}
+        done = set()
+        while len(done) < len(streams):
+            best = None
+            for n in streams:
+                if n in done or any(p not in done for p in streams[n][1]):
+                    continue
+                if pos[n] == len(streams[n][2]):
+                    done.add(n)
+                    best = None
+                    break
+                e, call, reads, writes, us = streams[n][2][pos[n]]
+                st = free[e]
+                w = deps(e, reads, writes)
+                for sem in w:
+                    st = max(st, when.get((sem, w[sem]), 0) + WAKE)
+                key = (round(st / 0.04), streams[n][0], st)
+                if best is None or key < best[0]:
+                    best = (key, n)
+            if best is not None:
+                n = best[1]
+                issue(*streams[n][2][pos[n]])
+                pos[n] += 1
+
+    def size(x):
+        return x[3].shape[1] if len(x) == 4 else 16 * x[1][3].shape[1]
+
+    def two(*xs):
+        return all(len(x) == 4 and (x[0] in HALF) for x in xs)
+
+    def dma(e, out, in_):
+        reads, writes = flat([in_]), flat([out])
+        need(e, reads, writes)
+        sem = "d%d" % dsem[0]
+        dsem[0] += 1
+        queue[e].dma_start(ap(out), ap(in_)).then_inc(T.sem[sem], 16)
+        free[e] += 0.1
+        when[(sem, 16)] = free[e] + (6.0 if out[0] in ("SNI", "X") else 3.0)
+        note(e, sem, 16, reads, writes)
+
+    def v(name, lo=0, hi=None, st=1, p=None):
+        buf, o, w = PLACE[name] if name in PLACE else (name, 0, SCRATCH[name][1][1])
+        t = T[buf]
+        if hi is None:
+            hi = w
+        ps = slice(None) if p is None else slice(*p)
+        return (name, lo, hi, t[ps, o + lo:o + hi] if st == 1 else t[ps, o + lo:o + hi:st])
+
+    def at(win, off):
+        return (win, off, win[3].indirect(off[3]))
+
+    def tc(out, in_):
+        sc, ga = len(out) == 3, len(in_) == 3
+        emit("v", lambda: g.vector.tensor_copy(ap(out), ap(in_)), [in_] + ([out[1]] if sc else []), [out[0] if sc else out],
+             0.05 + 3.8 * CY * size(out) if sc else 0.05 + 1.5 * CY * size(in_) if ga else CY * max(64, size(out) * (0.5 if two(out, in_) else 1)))
+
+    def tt(out, a, b, op):
+        emit("v", lambda: g.vector.tensor_tensor(ap(out), ap(a), ap(b), op), [a, b], [out],
+             0.05 + 1.5 * CY * size(a) if len(a) == 3 else CY * max(64, size(out) * (1 if a[0] in BANKS or b[0] in BANKS else 2)))
+
+    def ts(out, a, s1, op0, s2=None, op1=None):
+        us = CY * max(64, size(out) * (0.5 if two(out, a) else 1))
+        if op1 is None:
+            emit("v", lambda: g.vector.tensor_scalar(ap(out), ap(a), ap(s1), None, op0), [a, s1], [out], us)
+        else:
+            emit("v", lambda: g.vector.tensor_scalar(ap(out), ap(a), ap(s1), ap(s2), op0, op1), [a, s1, s2], [out], us)
+
+    def scan(out, d0, d1, op0, op1, init=0.0):
+        emit("v", lambda: g.vector.tensor_tensor_scan(ap(out), ap(d0), ap(d1), init, op0, op1), [d0, d1], [out], CY * max(64, size(out)))
+
+    def turn(out, in_):
+        emit("v", lambda: g.vector.transpose(ap(out), ap(in_)), [in_], [out], CY * max(64, size(out)))
+
+    def fill(out, c):
+        emit("v", lambda: g.vector.memset(ap(out), c), [], [out], CY * max(64, size(out)))
+
+    def act(out, in_, func=AF.Copy, bias=0.0):
+        us = 0.065 + 1.5 * CY * size(out) if len(in_) == 3 else CY * max(64, size(out))
+        if bias:
+            emit("s", lambda: g.scalar.activation(ap(out), ap(in_), func, bias=bias), [in_], [out], us)
+        else:
+            emit("s", lambda: g.scalar.activation(ap(out), ap(in_), func), [in_], [out], us)
+
+    def mm(out, lhsT, rhs, start, stop):
+        emit("t", lambda: g.tensor.matmul(ap(out), ap(lhsT), ap(rhs), start, stop), [lhsT, rhs], [out], CY * max(64, size(out)) * (1 if two(lhsT) else 4))
+
+    def iota(out, pattern, base, cm, small=False):
+        us = 0.15 + 2 * CY * size(out)
+        if small:
+            emit("g", lambda: g.iota(ap(out), pattern, base, cm, allow_small_or_imprecise_dtypes=True), [], [out], us)
+        else:
+            emit("g", lambda: g.iota(ap(out), pattern, base, cm), [], [out], us)
+
+    def pick(out, in_, pattern, op, base, cm):
+        emit("g", lambda: g.affine_select(ap(out), ap(in_), pattern, op, 0.0, base, cm), [in_], [out], 0.17 + 2 * CY * size(out))
+
+    add, sub, mul, eq, ne = OP.add, OP.subtract, OP.mult, OP.is_equal, OP.not_equal
+    ge, gt, lt = OP.is_ge, OP.is_gt, OP.is_lt
+
+    half = M // 2
+    dma("s", ("gnd", 0, M, T.gnd[:, 0:M]), ("gn", 0, M, T.gn[:]))
+    dma("s", ("gnd", W, Q * 3 + W, T.gnd[:, W:Q * 3 + W]), ("gn", 0, Q * 3, T.gn[:, 0:Q * 3]))
+    dma("y", v("SNI", 0, half), ("sn", 0, half, T.sn[:, 0:half]))
+    dma("y", v("SNI", half, M), ("sn", half, M, T.sn[:, half:M]))
+    dma("s", v("FGI", 0, M, p=(0, 8)), ("fa", 0, M, T.fa[:]))
+    dma("s", v("FGI", 0, M, p=(8, 16)), ("gn", 0, M, T.gn[:]))
+    dma("y", v("X", 0, M), ("x", 0, M, T.x[:]))
+    dma("y", v("WC"), ("w", 0, 1, T.w[:]))
+    fill(v("PAD", 0, 16), 0)
+    fill(v("PAD", 16, 208), 2)
+    dma("s", ("gnd", M, W, T.gnd[:, M:W]), v("PAD", p=(0, 8)))
+    for t in range(T_):
+        dma("s", v("GTI", 122 * t, 122 * (t + 1)), ("gnd", Q * t, Q * t + W, T.gnd[:, Q * t:Q * t + W]))
+
+    iota(v("PI"), [[1, 1]], 0, 1)
+    fill(v("ONES"), 1.0)
+    pick(v("TMPB"), v("ONES"), [[-16, 8], [0, 16]], ge, 0, 1)
+    pick(v("ONESB"), v("TMPB"), [[16, 8], [0, 16]], ge, 15, -1)
+    pick(v("TRI"), v("ONESB"), [[1, 128]], ge, -1, -1)
+    iota(v("RMOD"), [[0, 24], [1, 16]], 0, 0, True)
+    iota(v("POS"), [[1, 122]], 0, 0, True)
+    iota(v("D"), [[1, 122], [122, 16]], 0, 0, True)
+    ts(v("PI2"), v("PI"), 15, OP.bitwise_and)
+    tc(v("R16"), v("PI2"))
+    ts(v("PI2"), v("PI"), 4, OP.logical_shift_right, 1, OP.bitwise_and)
+    tc(v("PBF", 1, 2), v("PI2"))
+    ts(v("PBF", 0, 1), v("PBF", 1, 2), -1.0, mul, 1.0, add)
+    R16 = v("R16")
+    POSB, CQB, DIAGB = v("k4", 256, 378), v("k4", 384, 506), v("k3", 256, 448)
+    ts(v("R122"), R16, 122.0, mul)
+    ts(POSB, v("POS"), v("R122"), add)
+    ts(CQB, POSB, -1.0, mul, float(HWN), add)
+    fill(v("ZER"), 0.0)
+    fill(v("SEL"), 0.0)
+    for s in range(16):
+        ts(v("SEL", s * 128 + s, (s + 1) * 128, 16), v("ONESB", s, 128, 16), 16.0, mul)
+    fill(v("SN", M, 1760), float(M))
+    fill(v("SN", 1760, W), 0.0)
+    fill(v("SN", W, WT), float(M))
+    tc(v("SN", 0, half), v("SNI", 0, half))
+    tc(v("SN", half, M), v("SNI", half, M))
+    ts(v("GTH"), v("GTI"), 2, ge, -1.0, add)
+    iota(v("SLR"), [[0, 8], [1, 16]], 0, 0, True)
+    fill(v("OF"), 1.0)
+    for i, base in enumerate((0, 16, -16)):
+        pick(v("I3", 128 * i, 128 * (i + 1)), v("OF"), [[-1, 128]], eq, base, 1)
+    pick(v("LF", p=(0, 16)), v("OF", p=(0, 16)), [[1, 8], [0, 16]], eq, 0, -1)
+    fill(v("G2K"), 2048.0)
+    pick(v("LG", p=(0, 16)), v("G2K", p=(0, 16)), [[1, 8], [0, 16]], eq, 8, -1)
+    iota(v("VH8", p=(0, 1)), [[8, W // 8], [0, 8]], 0, 0, True)
+    iota(v("VL8", p=(0, 1)), [[0, W // 8], [1, 8]], 0, 0, True)
+    iota(v("LKI"), [[1, 64]], 0, 0)
+    iota(v("TRL"), [[16, 12]], L, 0, True)
+    iota(v("TR4"), [[0, 4], [16, 12]], TB, 0, True)
+    iota(v("COLC"), [[1, 64]], 1760, 0, True)
+
+    def constants_late():
+        tc(v("FGF", p=(0, 16)), v("FGI", p=(0, 16)))
+        ts(v("DIAG"), v("RMOD", 0, L), R16, eq)
+        ts(DIAGB, v("RMOD", 0, L), R16, eq)
+        ts(v("RS0"), v("RMOD"), 0.0, ne)
+        ts(v("RST"), v("RMOD", 0, 96), 0.0, eq, float(2 ** 20), mul)
+        fill(v("F1", M, 1760), float(M))
+        fill(v("F1", 1760, W + L), 0.0)
+        fill(v("F2", M, 1760), float(M))
+        fill(v("F2", 1760, W + L), 0.0)
+        fill(v("GH", M, W), 0.0)
+        fill(v("X", M, WT), BIG)
+        fill(v("X", 1760, W), 0.0)
+        w = M // 4
+        for j in range(4):
+            a, b = j * w, (j + 1) * w
+            k = "k%d" % (j % 2)
+            mm(v(k, 0, w), v("LF", p=(0, 16)), v("FGF", a, b, p=(0, 16)), True, True)
+            act(v("F1", a, b), v(k, 0, w))
+            act(v("F2", a, b), v(k, 0, w))
+        for e in range(2):
+            for y in range(2):
+                i = 0 if e == y else 1 if y else 2
+                ts(v("SW", 128 * (2 * e + y), 128 * (2 * e + y + 1)), v("I3", 128 * i, 128 * (i + 1)), v("PBF", e, e + 1), mul)
+        ts(v("TRL"), v("TRL"), R16, add)
+        ts(v("TR4"), v("TR4"), R16, add)
+        yield
+
+    def constants_last():
+        tc(v("FGB", p=(0, 16)), v("FGF", p=(0, 16)))
+        tc(v("LGB", p=(0, 16)), v("LG", p=(0, 16)))
+        w = M // 4
+        for j in range(4):
+            a, b = j * w, (j + 1) * w
+            k = "k%d" % (6 + j % 2)
+            mm(v(k, 0, w), v("LGB", p=(0, 16)), v("FGB", a, b, p=(0, 16)), True, False)
+            mm(v(k, 0, w), v("ONES", p=(0, 1)), v("VH8", a, b, p=(0, 1)), False, False)
+            mm(v(k, 0, w), v("ONES", p=(0, 1)), v("VL8", a, b, p=(0, 1)), False, True)
+            act(v("GH", a, b), v(k, 0, w))
+        ts(v("LTM"), v("RMOD"), R16, gt)
+        ts(v("D15"), v("DIAG"), -998.5, mul, 1000.0, add)
+        ts(v("M0"), R16, 0.0, eq)
+        ts(v("E0"), R16, 0.0, ne, float(M), mul)
+        for t in range(1, 4):
+            ts(v("MTC", t, t + 1), R16, float(t), eq)
+            ts(v("MTC", 4 + t, 5 + t), R16, float(t), ne)
+        tc(v("ONESF"), v("ONESB"))
+        tt(v("TRMO"), v("TRI"), v("ONESB"), sub)
+        ts(v("WSEL"), v("SEL"), v("WC"), mul, 0.0625, mul)
+        fill(v("BS0"), 0.0)
+        fill(v("BSA"), 0.0)
+        tc(v("LK"), v("LKI"))
+        yield
+
+    def narrow(src, n, tmp="TMP", res="RW"):
+        tt(v(tmp, 0, n), src, v("DIAG", 0, n) if src[0] in BANKS else v("k3", 256, 256 + n), mul)
+        scan(v(res, 0, n), v("RS0", 0, n), v(tmp, 0, n), mul, add)
+        return v(res, 15, n, 16)
+
+    def lanes1(t):
+        c = W // 4
+        st = Q * t
+        segs = [(a, min(a + c, W)) for a in range(0, W, c)]
+        k0 = st // c
+        fill(v("HWIN", 0, L), float(M))
+        for a, b in segs[k0:] + segs[:k0]:
+            act(v("ANE", a, b), v("SN", a, b), AF.Abs, -float(M))
+        for m in range(16):
+            a = st + 122 * m
+            parts = [(a, a + 122)] if a + 122 <= W or a >= W else [(a, W), (W, a + 122)]
+            for x, y in parts:
+                mm(v("k6", x - a, y - a), v("SEL", 128 * m, 128 * (m + 1)), v("ANE", x % W, x % W + y - x), m == 0, m == 15)
+        tt(v("NOK"), v("k6", 0, 122), v("GTH", 122 * t, 122 * (t + 1)), gt)
+        scan(v("NINC"), v("NOK"), v("ZER"), add, add)
+        mm(v("k7", 0, 1), v("TRI"), v("NINC", 121, 122), True, True)
+        tt(v("C1"), v("NOK"), CQB, mul)
+        tt(v("k3", 0, 122), v("C1"), POSB, add)
+        tt(v("C1"), v("k3", 0, 122), v("NINC"), sub)
+        ts(v("OFF16"), v("C1"), v("k7", 0, 1), sub)
+        tc(at(v("HWIN"), v("OFF16")), v("D"))
+        if t < 3:
+            iota(v("D"), [[1, 122], [122, 16]], Q * (t + 1), 0, True)
+        yield
+
+    def lanes2(t):
+        if t:
+            ts(v("k4", 0, L), v("HWIN", 0, L), float(W), ge, -float(W), mul)
+            tt(v("H"), v("k4", 0, L), v("HWIN", 0, L), add)
+        else:
+            tc(v("H"), v("HWIN", 0, L))
+        F = "F1" if t % 2 == 0 else "F2"
+        tab = v("SN")
+        r = narrow(v("H"), L)
+        tc(v("HL"), r)
+        tc(v("P0"), at(v(F, 0, W), v("HL")))
+        tc(v("H16"), v("H"))
+        tc(v("HW12"), r)
+        act(v("XR", 0, 1536), at(v("X"), v("H16", 0, 96)))
+        act(v("XR", 1536, 3072), at(v("X"), v("H16", 96, 192)))
+        r = narrow(v("P0"), L)
+        tc(v("P0L"), r)
+        tc(v("P0W"), r)
+        tc(v("S0"), at(tab, v("P0L")))
+        tc(v("P1"), at(v(F, 0, W), v("P0L")))
+        tt(v("EQ0"), v("S0"), v("H"), eq)
+        ts(v("EM0"), v("S0"), float(M), eq)
+        mm(v("k6", 0, L), v("ONESB"), v("EQ0"), True, False)
+        mm(v("k6", 0, L), v("ONESB"), v("EM0"), False, True)
+        r = narrow(v("P1"), L)
+        tc(v("P1L"), r)
+        tc(v("S1"), at(tab, v("P1L")))
+        ts(v("k5", 128, 320), v("EQ0"), float(BK), mul)
+        tt(v("W0"), v("k5", 128, 320), v("S0"), add)
+        tt(v("EQ1"), v("S1"), v("P0"), eq)
+        ts(v("k5", 128, 320), v("EQ1"), float(BK), mul)
+        tt(v("k4", 0, L), v("k5", 128, 320), v("S1"), add)
+        tt(v("WD"), v("k4", 0, L), v("W0"), sub)
+        ts(v("k5", 320, 512), v("k6", 0, L), 16.0, ge)
+        tt(v("k4", 0, L), v("WD"), v("k5", 320, 512), mul)
+        tt(v("SA"), v("k4", 0, L), v("W0"), add)
+        tc(v("SA16"), v("SA"))
+        yield
+
+    def own_flags(t):
+        act(v("XL"), at(v("X"), v("HL")))
+        r = narrow(v("k5", 320, 512), L)
+        if t < 3:
+            act(v("HG"), at(v("GH"), v("HL")))
+        tc(v("U2", 0, 12), r)
+        tc(v("U2", 12, 24), r)
+        ts(v("ND"), v("P0W"), 64.0, lt)
+        tt(v("ND"), v("ND"), v("U2", 0, 12), mul)
+        ts(v("ND"), v("ND"), -1.0, mul, 1.0, add)
+        tc(v("Z4", 0, 12), v("HW12"))
+        if t < 3:
+            ts(v("LOF"), v("HW12"), float(M), ne)
+            fill(v("ms%d" % t, 0, 384), 0.0)
+            fill(v("HGS%d" % t, 0, 384), 0.0)
+        yield
+
+    def down(tag, nq, idx, son, offl, xr, u, u0, lst, keep=None, cuts=2):
+        n = nq * 16
+        kb, vb = {"A1": ("k0", "k3"), "A2": ("k1", "k4"), "AB": ("k2", "k5")}[tag]
+        c = n // cuts
+        for j in range(cuts):
+            a, b = j * c, (j + 1) * c
+            ux = v(u, u0 + 16 * a, u0 + 16 * b)
+            tt(ux, at(v("X"), v(idx, offl + a, offl + b)), v(xr, u0 + 16 * a, u0 + 16 * b), sub)
+            act(ux, ux, AF.Abs)
+            for s in range(16):
+                mm(v(kb, a, b), v("SEL", 128 * s, 128 * (s + 1)), v(u, u0 + 16 * a + s, u0 + 16 * b, 16), s == 0, False)
+            mm(v(kb, a, b), v("SLR", p=(0, 1)), v("ONES", 0, c, p=(0, 1)), False, True)
+        SP, KP = v(vb, 0, n), v(vb, n, 2 * n) if tag == "AB" else v(vb, 128, 128 + n)
+        turn(SP, son)
+        turn(KP, v(kb, 0, n))
+        im, ni, zz, rr = [v(x + tag, 0, n) for x in ("IM", "NI", "ZZ", "RR")]
+        mm_ = v("MM" + tag, 0, n) if keep is None else v("MKEEP", keep, keep + n)
+        scan(mm_, v("RST", 0, n), KP, add, OP.min, float(2 ** 20))
+        tt(im, mm_, KP, eq)
+        tt(ni, mm_, KP, ne)
+        tt(zz, im, SP, mul)
+        scan(rr, ni, zz, mul, add)
+        for e in range(2):
+            for y in range(2):
+                mm(v(kb, 288 + e, 288 + nq, 2), v("SW", 128 * (2 * e + y), 128 * (2 * e + y + 1)), v("RR" + tag, 15 + 16 * y, n, 32), y == 0, y == 1)
+        lst(v(kb, 288, 288 + nq))
+
+    def own(h):
+        tag, o, lo = ("A1", 0, 0) if h == 0 else ("A2", 6, 96)
+
+        def after(step, name):
+            def f(x):
+                if step < 2:
+                    tc(v(name, o, o + 6), x)
+                act(v("WALL", 12 * step + o, 12 * step + o + 6), x)
+            return f
+        down(tag, 6, "SA16", v("SA", lo, lo + 96), lo, "XR", "UA", 1536 * h, after(0, "LA"))
+        for step, prev, name in ((1, "LA", "LB"), (2, "LB", "")):
+            tc(v("S16A", lo, lo + 96), at(v("SN"), v(prev, o, o + 6)))
+            act(v("SF" + tag), at(v("SN"), v(prev, o, o + 6)))
+            down(tag, 6, "S16A", v("SF" + tag), lo, "XR", "UA", 1536 * h, after(step, name), keep=192 * (step - 1) + lo)
+        yield
+
+    def arrivals(t):
+        ls = "ls%d" % (t - 1)
+        for r in range(16):
+            mm(v("k2", 0, 4), v("WSEL", 128 * r, 128 * (r + 1)), v(ls, r, S, 16), r == 0, r == 15)
+        act(v("XRB"), at(v(ls, 0, S), v("LK")))
+        tc(v("CI"), v("k2", 0, 4))
+        for d in range(3):
+            ts(v("GENM", 4 * d, 4 * d + 4), v(ls, S, SW_), float(d + 2), eq)
+        ts(v("CI2"), v("CI"), 63, OP.bitwise_and)
+        tc(v("BL"), v("CI2"))
+        for e in range(4):
+            tc(v("S16B"), at(v("SN"), v("BL")))
+            act(v("SFAB"), at(v("SN"), v("BL")))
+
+            def f(x):
+                if e < 3:
+                    tc(v("BL"), x)
+                if e:
+                    act(v("LB3", 4 * (e - 1), 4 * e), x)
+            down("AB", 4, "S16B", v("SFAB"), 0, "XRB", "UB", 0, f, cuts=1)
+        ts(v("LBT"), v("LB3"), -float(M), add)
+        tt(v("LB3"), v("LBT"), v("GENM"), mul)
+        tt(v("LBT", 0, 4), v("LB3", 0, 4), v("LB3", 4, 8), add)
+        tt(v("LBT", 4, 8), v("LBT", 0, 4), v("LB3", 8, 12), add)
+        ts(v("BF16"), v("LBT", 4, 8), float(M), add)
+        tc(v("mr%d" % t), at(v("X"), v("BF16")))
+        ship("r", t, v("mr%d" % t))
+        yield
+
+    sent = [0]
+
+    def ship(kind, t, src):
+        k = "%s%d" % (kind, t)
+        dst = goal(T, rank, kind, t)
+        mid = via(topo, core, dst)
+
+        def call():
+            if mid is None:
+                send(g, topo, core, dst, T["l" + k][:], src[3], T.sem["a" + k], T.sem.lo)
+            else:
+                send(g, topo, core, mid, T["b" + k][:], src[3], T.sem["x" + k], T.sem.lo)
+            sent[0] += NENG
+            when[("a" + k, NENG)] = free["g"] + 6.0
+        emit("g", call, [src], [], 1.0)
+
+    def found(t):
+        tt(v("D1"), v("WALL", 12, 36), v("WALL", 0, 24), sub)
+        tt(v("YT"), v("D1"), v("U2"), mul)
+        tt(v("YS"), v("YT"), v("WALL", 0, 24), add)
+        ts(v("YT", 0, 12), v("YS", 12, 24), float(M), ne)
+        tt(v("FND", 0, 12), v("YT", 0, 12), v("ND"), mul)
+        tt(v("FND", 12, 24), v("YT", 0, 12), v("ND"), mul)
+        if t < 3:
+            tt(v("LO"), v("LOF"), v("FND", 0, 12), sub)
+            tt(v("LOF"), v("LOF"), v("FND", 0, 12), sub)
+            mm(v("k0", 256, 268), v("ONESB"), v("LO"), True, True)
+            mm(v("k0", 272, 284), v("TRMO"), v("LO"), True, True)
+        yield
+
+    def adopt(t):
+        ts(v("D1"), v("YS"), 1.0, add)
+        tc(v("YL"), v("YS", 0, 12))
+        tt(v("YT"), v("D1"), v("FND"), mul)
+        tc(v("SL"), v("YS", 12, 24))
+        ts(v("BS0", 0, 384, 16), v("YT"), -1.0, add)
+        scan(v("SCB"), v("RS0"), v("BS0"), mul, add)
+        tt(v("DX", 0, L), v("SCB", 0, L), DIAGB, mul)
+        mm(v("k7", 0, L), v("ONESF"), v("DX", 0, L), True, True)
+        tt(v("DX", L, 384), v("SCB", L, 384), DIAGB, mul)
+        mm(v("k7", L, 384), v("ONESF"), v("DX", L, 384), True, True)
+        tc(v("SY"), at(v("SN"), v("YL")))
+        act(v("Z4", 12, 24), v("YS", 12, 24))
+        act(v("Z4", 24, 36), v("YS", 0, 12))
+        act(v("Z4", 36, 48), v("YS", 12, 24))
+        ts(v("EMY"), v("SY"), float(M), ne)
+        mm(v("k1", 0, L), v("ONESB"), v("EMY"), True, True)
+        tt(v("Z5"), v("Z4"), v("TR4"), sub)
+        tc(v("YR16"), v("k7", 0, 384))
+        tt(v("k5", 128, 512), v("SCB"), v("k7", 0, 384), eq)
+        tt(v("EDM"), v("k5", 128, 512), v("LTM"), mul)
+        mm(v("k6", 0, L), v("ONESB"), v("EDM", 0, L), True, False)
+        mm(v("k6", 0, L), v("ONESB"), v("EDM", L, 384), False, False)
+        o = 0
+        for q in range(11):
+            n = (11 - q) * 16
+            for z in range(2):
+                ts(v("EE", o, o + n), v("YR16", L * z + L - n, L * z + L), v("BS0", L * z + 16 * q, L * z + 16 * q + 1), eq)
+                mm(v("k6", L - n, L), v("ONESB"), v("EE", o, o + n), False, q == 10 and z == 1)
+                o += n
+        tt(v("SR"), v("D15"), v("k1", 0, L), lt)
+        scan(v("SRS"), v("RS0", 0, L), v("SR"), mul, add)
+        tt(v("FR"), v("DIAG"), v("k6", 0, L), gt)
+        scan(v("FRS"), v("RS0", 0, L), v("FR"), mul, add)
+        tt(v("FL4", 0, 12), v("FRS", 15, L, 16), v("FND", 0, 12), mul)
+        tt(v("FL4", 12, 24), v("FRS", 15, L, 16), v("FND", 0, 12), mul)
+        tt(v("FL4", 24, 36), v("SRS", 15, L, 16), v("FL4", 0, 12), mul)
+        tt(v("FL4", 36, 48), v("SRS", 15, L, 16), v("FL4", 0, 12), mul)
+        tt(v("Z4"), v("Z5"), v("FL4"), mul)
+        tt(v("Z5"), v("Z4"), v("TR4"), add)
+        tc(v("L4"), v("Z5"))
+        yield
+
+    def slots(t):
+        for e in range(2):
+            for y in range(2):
+                mm(v("k2", 256 + e, 280, 2), v("SW", 128 * (2 * e + y), 128 * (2 * e + y + 1)), v("MKEEP", 15 + 16 * y, 384, 32), y == 0, y == 1)
+        act(v("KALL"), v("k2", 256, 280))
+        tt(v("KF"), v("KALL", 12, 24), v("KALL", 0, 12), sub)
+        tt(v("AW"), v("KF"), v("U2", 0, 12), mul)
+        tt(v("KF"), v("AW"), v("KALL", 0, 12), add)
+        tc(v("KI"), v("KF"))
+        ts(v("KI2"), v("KI"), 15, OP.bitwise_and)
+        tc(v("BSA", 0, L, 16), v("KI2"))
+        scan(v("k4", 0, L), v("RS0", 0, L), v("BSA"), mul, add)
+        tt(v("AX"), v("k4", 0, L), v("DIAG"), mul)
+        mm(v("k0", 0, L), v("ONESB"), v("AX"), True, True)
+        yield
+
+    def change_sons(t):
+        ts(v("VH"), v("k7", L, 384), v("M0"), mul, v("E0"), add)
+        ts(v("DD"), v("SY"), -1.0, mul, float(M), add)
+        ts(v("k1", 0, L), v("k0", 0, L), R16, eq)
+        tc(at(v("SN", 0, W + L), v("L4", 0, 12)), v("VH"))
+        tt(v("k3", 0, L), v("DD"), v("k1", 0, L), mul)
+        tt(v("VY"), v("k3", 0, L), v("SY"), add)
+        tc(at(v("SN", 0, W + L), v("L4", 24, 36)), v("VY"))
+        yield
+
+    def sending(t):
+        ms, hg = "ms%d" % t, "HGS%d" % t
+        scan(v("CS"), v("k0", 256, 268), v("ZER", 0, 12), add, add)
+        tt(v("DA"), v("CS"), v("k0", 272, 284), add)
+        tt(v("DB"), v("DA"), v("TRL"), sub)
+        tt(v("DA"), v("DB"), v("LOF"), mul)
+        tt(v("DB"), v("DA"), v("TRL"), add)
+        tc(v("LO16"), v("DB"))
+        tc(at(v(hg), v("LO16")), v("HG"))
+        tc(at(v(ms), v("LO16")), v("XL"))
+        r = narrow(v(hg, 0, S), S, "RT", "RTS")
+        tc(v("HI4"), r)
+        ts(v("HI4B"), v("HI4"), 11, OP.logical_shift_right)
+        tc(v(ms, S, SW_), v("HI4B"))
+        ship("s", t, v(ms, 0, SW_))
+        ts(v("HI4B"), v("HI4"), 2047, OP.bitwise_and)
+        tc(v("HSW%d" % t), v("HI4B"))
+        tc(v("HS%d" % t), v("HI4B"))
+        yield
+
+    def change_rest(t):
+        tt(v("XG"), at(v("X"), v("SL")), v("XL"), add)
+        ts(v("XG"), v("XG"), 0.5, sub, 0.5, mul)
+        tc(v("XI"), v("XG"))
+        tc(at(v("X", 0, W + L), v("L4", 12, 24)), v("XI"))
+        tc(at(v("F2"), v("L4", 12, 24)), v("H"))
+        tc(at(v("F1"), v("L4", 36, 48)), v("H"))
+        yield
+
+    def guests(t):
+        if t >= 1:
+            lr, a = "lr%d" % t, 1760 + S * (t - 1)
+            tt(v("X", a, a + S), v(lr), v("FD"), mul)
+            tt(v("F1", a, a + S), v("HROW%d" % (t - 1)), v("FD"), mul)
+            tt(v("F2", a, a + S), v("HROW%d" % (t - 1)), v("FD"), mul)
+            if t < 3:
+                tc(v("GH", a, a + S), v("GHN%d" % (t - 1)))
+        yield
+
+    def note_sent(t):
+        hg = "HGS%d" % t
+        tc(v("HIR"), v(hg, 0, S))
+        ts(v("HIR2"), v("HIR"), 2047, OP.bitwise_and)
+        tc(v("HROW%d" % t), v("HIR2"))
+        tt(v("RV"), v(hg, 0, S), v("HROW%d" % t), sub)
+        ts(v("RV2"), v("RV"), 2048.0 + S * t, add)
+        tt(v("GHN%d" % t), v("RV2"), v("COLC"), add)
+        yield
+
+    def returns(t):
+        lr, a = "lr%d" % t, 1760 + S * (t - 1)
+        hw, hs = "HSW%d" % (t - 1), "HS%d" % (t - 1)
+        ts(v("FD"), v(lr), 256.0, lt)
+        if t < 3:
+            r = narrow(v("FD"), S, "RTB", "RTSB")
+            tt(v("RZ"), v(hw), v("TR4", 0, 4), sub)
+            tc(v("RVB"), at(v("SN", 0, W), v(hs)))
+            tt(v("FDW"), v("RZ"), r, mul)
+            ts(v("RV2B"), v("RVB"), v("MTC", 4 + t, 5 + t), mul)
+            tt(v("RZ"), v("FDW"), v("TR4", 0, 4), add)
+            ts(v("RTB"), v("COLC"), float(S * (t - 1)), add, v("MTC", t, t + 1), mul)
+            tc(v("RL16"), v("RZ"))
+            tt(v("RVB"), v("RV2B"), v("RTB"), add)
+            ts(v("SN", a, a + S), v(lr), 256.0, lt, float(M), mul)
+            tc(at(v("SN", 0, W + L), v("RL16")), v("RVB"))
+        yield
+
+    for kind, t in MSGS:
+        k = "%s%d" % (kind, t)
+        wr["l" + k] = [(0, 1 << 20, "remote", "a" + k, NENG)]
+        total["a" + k] = NENG
+    st = {"late": (3, [], record(constants_late()))}
+    for t in range(T_):
+        p, last = "%d" % t, "%d" % (t - 1)
+        st["lanes1" + p] = (1, ["returns" + last] if t else [], record(lanes1(t)))
+        st["lanes2" + p] = (1, ["lanes1" + p] + (["rest" + last, "guests" + last, "sending" + last] if t else ["late"]), record(lanes2(t)))
+        if t:
+            st["arrivals" + p] = (0, ["rest" + last, "guests" + last, "returns" + last], record(arrivals(t)))
+        else:
+            st["last"] = (6, ["lanes2" + p], record(constants_last()))
+        st["own0" + p] = (2, ["lanes2" + p], record(own(0)))
+        st["own1" + p] = (3, ["lanes2" + p], record(own(1)))
+        st["flags" + p] = (4, ["lanes2" + p, "last"], record(own_flags(t)))
+        st["found" + p] = (1, ["own0" + p, "own1" + p, "flags" + p], record(found(t)))
+        st["adopt" + p] = (1, ["found" + p], record(adopt(t)))
+        over = ["adopt" + p] + (["arrivals" + p] if t else [])
+        if t < 3:
+            st["slots" + p] = (2, ["found" + p] + (["arrivals" + p] if t else []), record(slots(t)))
+            st["sending" + p] = (3, ["found" + p], record(sending(t)))
+            st["sons" + p] = (1, over + ["slots" + p], record(change_sons(t)))
+            st["noted" + p] = (5, ["sending" + p], record(note_sent(t)))
+        st["returns" + p] = (2, (["sons" + p] if t < 3 else over) + (["noted" + last] if t else []), record(returns(t)) if t else [])
+        st["rest" + p] = (4, over, record(change_rest(t)))
+        st["guests" + p] = (4, ["rest" + p, "returns" + p], record(guests(t)))
+    merge(st)
+
+    fill(v("F1", M, 1760), 0.0)
+    fill(v("F2", M, 1760), 0.0)
+    fill(v("X", M, 1760), 0.0)
+    dma("s", ("fo", 0, W, T.fo[:]), v("F1", 0, W, p=(0, 128, 16)))
+    dma("y", ("xo", 0, W, T.xo[:]), v("X", 0, W))
+    dma("s", ("f2o", 0, W, T.f2o[:]), v("F2", 0, W, p=(0, 128, 16)))
+    for sem in sorted(total):
+        g.wait_ge(T.sem[sem], total[sem])
+    g.wait_ge(T.sem.lo, sent[0])

@@ -2,23 +2,24 @@ from concourse.mybir import AluOpType as OP, ActivationFunctionType as AF
 
 M, W, L, S, T_, Q = 1744, 1952, 192, 64, 4, 560
 BK = 2176
-WT = BK + W
-TB = W
+WT = BK + W + 32
 HWN = W + L
+TB = W
 BIG = 512.0
 SW_ = 68
 NENG = 8
+NV = {"A0": 48, "A1": 48, "A2": 64, "AB": 48}
 
 SCRATCH = {}
 PLACE = {}
 HALF = set()
 BANKS = set("k%d" % i for i in range(8))
-POOL = {"float32": ["poolf", 0], "bfloat16": ["poolh", 0], "int32": ["pooli", 0], "uint16": ["poolu", 0]}
+POOL = {"float32": ["poolf", 0], "float16": ["poole", 0], "bfloat16": ["poolh", 0], "int32": ["pooli", 0], "uint16": ["poolu", 0]}
 
 
 def _b(kind, dtype, **kw):
     for n, w in kw.items():
-        if dtype in ("bfloat16", "uint16"):
+        if dtype in ("bfloat16", "uint16", "float16"):
             HALF.add(n)
         if kind == "psum" or n[:2] in ("ms", "bs", "ls", "mr", "br", "lr"):
             SCRATCH[n] = (kind, [128, w], dtype)
@@ -29,25 +30,30 @@ def _b(kind, dtype, **kw):
             SCRATCH[p[0]] = (kind, [128, p[1]], dtype)
 
 
-_b("sbuf", "float32", SN=WT, F1=W + L, F2=W + L, GH=W, HWIN=HWN, D=W, H=L, TMP=L, RW=L, P0=L, P1=L, S0=L, S1=L, W0=L,
-   WD=L, SA=L, HG=L, RMOD=384, DIAG=L, LTM=384, RS0=384, RST=96, D15=L, OF=128, I3=384, SW=512, ONESF=128,
-   R16=1, PBF=2, R122=1, M0=1, E0=1, TRL=12, TR4=48, POS=122, COLC=64, ZER=122, GTH=488, NOK=122, C1=122,
-   HW12=12, P0W=12, U2=24, ND=12, WALL=36, KALL=24, D1=24, YS=24, KF=12, AW=12, FND=24, YT=24, BS0=384, SCB=384,
-   DX=384, BSA=L, FR=L, FRS=L, SR=L, SRS=L, FL4=48, Z4=48, Z5=48, SY=L, DD=L, VH=L, VY=L, XG=L, LOF=12,
+_b("sbuf", "float32", SN=WT, F1=W + L, F2=W + L, GH=W, H=L, TMP=L, RW=L, P0=L, P1=L, SA=L, HG=L, RMOD=384, DIAG=L, LTM=384, RS0=384, RST=96, D15=L, OF=128, I3=384, SW=512,
+   R16=1, PBF=2, M0=1, E0=1, TRL=12, TR4=48, COLC=64, ZER=122, HW12=12, P0W=12, U2=24, ND=12, WALL=36, KALL=24, D1=24, YS=24, KF=12, AW=12, FND=24, YT=24, BS0=384, SCB=384,
+   BSA=L, FR=L, FRS=L, SR=L, SRS=L, FL4=48, Z4=48, Z5=48, SY=L, DD=L, VH=L, VY=L, XG=L, LOF=12,
    CS=12, DA=12, DB=12, RT=S, RTS=S, RTB=S, RTSB=S, FDW=4, RZ=4, RV=S, RV2=S, RVB=S, RV2B=S, FD=S, GENM=12, LB3=12, LBT=12,
-   LF=128, LG=128, G2K=128, FGF=M, MTC=8, MKEEP=384)
-for _n in ("A1", "A2", "AB"):
-    _w = 64 if _n == "AB" else 96
-    _b("sbuf", "float32", **{"SF" + _n: _w, "MM" + _n: _w, "IM" + _n: _w, "NI" + _n: _w, "ZZ" + _n: _w, "RR" + _n: _w})
+   LFF=128, LG=128, G2K=128, MTC=8, MKEEP=384)
+for _n in ("A0", "A1", "A2", "AB"):
+    _b("sbuf", "float32", **{"SF" + _n: 64, "MM" + _n: 64, "IM" + _n: 64, "NI" + _n: 64, "ZZ" + _n: 64})
+    _b("sbuf", "float16", **{"RR" + _n: 64})
+_b("sbuf", "float16", SWH=512, ONESH=128, DX=384, FGF=M, LF=128, IDH=128, NIDH=128, S0=L, S1=L)
+_b("sbuf", "bfloat16", IDK=128, NIDK=128, UR=L, EC=1056, EZ=1056)
+_b("sbuf", "float32", UD=L, SROW=L)
+SCRATCH["gnd"] = ("dram", [8, Q * 3 + W], "int32")
+_b("sbuf", "float32", HWIN=HWN, D=W, R122=1, POS=122, GTH=488, NOK=122, C1=122)
+_b("sbuf", "bfloat16", NINC=122, IDB=128, NIDB=128)
+_b("sbuf", "int32", GTI=488, PAD=208)
+_b("sbuf", "uint16", OFF16=122)
 _b("sbuf", "bfloat16", X=WT, ANE=W, SEL=2048, WSEL=2048, ONES=128, ONESB=128, TRI=128, TRMO=128, SLR=128, XL=L, XR=3072,
-   XRB=1024, UA=3072, UB=1024, EQ0=L, EM0=L, EQ1=L, NINC=122, EDM=384, EE=2112, EMY=L, AX=L, LO=12, WC=1, TMPB=128,
+   XRB=1024, UA=3072, UB=1024, EQ0=L, EM0=L, EQ1=L, EDM=384, EE=2112, EMY=L, AX=L, LO=12, WC=1, TMPB=128,
    FGB=M, LGB=128, VH8=W, VL8=W)
-_b("sbuf", "int32", SNI=M, FGI=M, GTI=488, PI=1, PI2=1, PAD=208, LKI=64, KI=12, KI2=12, HI4=4, HI4B=4, HIR=S, HIR2=S,
+_b("sbuf", "int32", SNI=M, FGI=M, PI=1, PI2=1, LKI=64, KI=12, KI2=12, HI4=4, HI4B=4, HIR=S, HIR2=S,
    CI=4, CI2=4, XI=L)
-_b("sbuf", "uint16", OFF16=122, H16=L, HL=12, P0L=12, P1L=12, SA16=L, S16B=64, S16A=L, LA=12, LB=12, LK=64, BL=4,
+_b("sbuf", "uint16", H16=L, HL=12, P0L=12, P1L=12, SA16=L, S16B=64, S16A=L, LA=12, LB=12, LK=64, BL=4,
    YR16=384, YL=12, SL=12, L4=48, LO16=12, RL16=4, BF16=4)
 _b("psum", "float32", k0=512, k1=512, k2=512, k3=512, k4=512, k5=512, k6=512, k7=512)
-SCRATCH["gnd"] = ("dram", [8, Q * 3 + W], "int32")
 for _t in range(3):
     _b("sbuf", "bfloat16", **{"ms%d" % _t: 384, "bs%d" % _t: SW_, "ls%d" % _t: SW_, "mr%d" % (_t + 1): S, "br%d" % (_t + 1): S, "lr%d" % (_t + 1): S})
     _b("sbuf", "float32", **{"HGS%d" % _t: 384, "HROW%d" % _t: S, "GHN%d" % _t: S, "HSW%d" % _t: 4})
@@ -267,10 +273,10 @@ def rank_program(g, core, T, topo):
     def fill(out, c):
         emit("v", lambda: g.vector.memset(ap(out), c), [], [out], CY * max(64, size(out)))
 
-    def act(out, in_, func=AF.Copy, bias=0.0):
+    def act(out, in_, func=AF.Copy, bias=0.0, scale=1.0):
         us = 0.065 + 1.5 * CY * size(out) if len(in_) == 3 else CY * max(64, size(out))
-        if bias:
-            emit("s", lambda: g.scalar.activation(ap(out), ap(in_), func, bias=bias), [in_], [out], us)
+        if bias != 0.0 or scale != 1.0:
+            emit("s", lambda: g.scalar.activation(ap(out), ap(in_), func, bias=ap(bias), scale=scale), [in_, bias], [out], us)
         else:
             emit("s", lambda: g.scalar.activation(ap(out), ap(in_), func), [in_], [out], us)
 
@@ -299,6 +305,7 @@ def rank_program(g, core, T, topo):
     dma("s", v("FGI", 0, M, p=(8, 16)), ("gn", 0, M, T.gn[:]))
     dma("y", v("X", 0, M), ("x", 0, M, T.x[:]))
     dma("y", v("WC"), ("w", 0, 1, T.w[:]))
+
     fill(v("PAD", 0, 16), 0)
     fill(v("PAD", 16, 208), 2)
     dma("s", ("gnd", M, W, T.gnd[:, M:W]), v("PAD", p=(0, 8)))
@@ -337,18 +344,19 @@ def rank_program(g, core, T, topo):
     fill(v("OF"), 1.0)
     for i, base in enumerate((0, 16, -16)):
         pick(v("I3", 128 * i, 128 * (i + 1)), v("OF"), [[-1, 128]], eq, base, 1)
-    pick(v("LF", p=(0, 16)), v("OF", p=(0, 16)), [[1, 8], [0, 16]], eq, 0, -1)
     fill(v("G2K"), 2048.0)
     pick(v("LG", p=(0, 16)), v("G2K", p=(0, 16)), [[1, 8], [0, 16]], eq, 8, -1)
-    iota(v("VH8", p=(0, 1)), [[8, W // 8], [0, 8]], 0, 0, True)
-    iota(v("VL8", p=(0, 1)), [[0, W // 8], [1, 8]], 0, 0, True)
-    iota(v("LKI"), [[1, 64]], 0, 0)
+    pick(v("LFF", p=(0, 16)), v("OF", p=(0, 16)), [[1, 8], [0, 16]], eq, 0, -1)
     iota(v("TRL"), [[16, 12]], L, 0, True)
     iota(v("TR4"), [[0, 4], [16, 12]], TB, 0, True)
+    iota(v("LKI"), [[1, 64]], 0, 0)
     iota(v("COLC"), [[1, 64]], 1760, 0, True)
+    iota(v("VH8", p=(0, 1)), [[8, W // 8], [0, 8]], 0, 0, True)
+    iota(v("VL8", p=(0, 1)), [[0, W // 8], [1, 8]], 0, 0, True)
 
     def constants_late():
         tc(v("FGF", p=(0, 16)), v("FGI", p=(0, 16)))
+        tc(v("LF", p=(0, 16)), v("LFF", p=(0, 16)))
         ts(v("DIAG"), v("RMOD", 0, L), R16, eq)
         ts(DIAGB, v("RMOD", 0, L), R16, eq)
         ts(v("RS0"), v("RMOD"), 0.0, ne)
@@ -363,25 +371,32 @@ def rank_program(g, core, T, topo):
         w = M // 4
         for j in range(4):
             a, b = j * w, (j + 1) * w
-            k = "k%d" % (j % 2)
+            k = "k%d" % (2 * (j % 2))
             mm(v(k, 0, w), v("LF", p=(0, 16)), v("FGF", a, b, p=(0, 16)), True, True)
             act(v("F1", a, b), v(k, 0, w))
-            act(v("F2", a, b), v(k, 0, w))
         for e in range(2):
             for y in range(2):
                 i = 0 if e == y else 1 if y else 2
                 ts(v("SW", 128 * (2 * e + y), 128 * (2 * e + y + 1)), v("I3", 128 * i, 128 * (i + 1)), v("PBF", e, e + 1), mul)
+        tc(v("SWH"), v("SW"))
+        act(v("IDB"), v("I3", 0, 128))
+        act(v("NIDB"), v("I3", 0, 128), scale=-1.0)
+        act(v("IDK"), v("I3", 0, 128), scale=float(BK))
+        act(v("NIDK"), v("I3", 0, 128), scale=-float(BK))
+        tc(v("IDH"), v("I3", 0, 128))
+        ts(v("NIDH"), v("I3", 0, 128), -1.0, mul)
         ts(v("TRL"), v("TRL"), R16, add)
         ts(v("TR4"), v("TR4"), R16, add)
         yield
 
     def constants_last():
-        tc(v("FGB", p=(0, 16)), v("FGF", p=(0, 16)))
+        tc(v("FGB", p=(0, 16)), v("FGI", p=(0, 16)))
         tc(v("LGB", p=(0, 16)), v("LG", p=(0, 16)))
+        act(v("F2", 0, M), v("F1", 0, M))
         w = M // 4
         for j in range(4):
             a, b = j * w, (j + 1) * w
-            k = "k%d" % (6 + j % 2)
+            k = "k2"
             mm(v(k, 0, w), v("LGB", p=(0, 16)), v("FGB", a, b, p=(0, 16)), True, False)
             mm(v(k, 0, w), v("ONES", p=(0, 1)), v("VH8", a, b, p=(0, 1)), False, False)
             mm(v(k, 0, w), v("ONES", p=(0, 1)), v("VL8", a, b, p=(0, 1)), False, True)
@@ -389,11 +404,12 @@ def rank_program(g, core, T, topo):
         ts(v("LTM"), v("RMOD"), R16, gt)
         ts(v("D15"), v("DIAG"), -998.5, mul, 1000.0, add)
         ts(v("M0"), R16, 0.0, eq)
-        ts(v("E0"), R16, 0.0, ne, float(M), mul)
+        ts(v("E0"), R16, 0.0, ne, float(M + 1), mul)
+        ts(v("E0"), v("E0"), -1.0, add)
         for t in range(1, 4):
             ts(v("MTC", t, t + 1), R16, float(t), eq)
             ts(v("MTC", 4 + t, 5 + t), R16, float(t), ne)
-        tc(v("ONESF"), v("ONESB"))
+        tc(v("ONESH"), v("ONESB"))
         tt(v("TRMO"), v("TRI"), v("ONESB"), sub)
         ts(v("WSEL"), v("SEL"), v("WC"), mul, 0.0625, mul)
         fill(v("BS0"), 0.0)
@@ -409,7 +425,7 @@ def rank_program(g, core, T, topo):
     def lanes1(t):
         c = W // 4
         st = Q * t
-        segs = [(a, min(a + c, W)) for a in range(0, W, c)]
+        segs = [(a, a + c) for a in range(0, W, c)]
         k0 = st // c
         fill(v("HWIN", 0, L), float(M))
         for a, b in segs[k0:] + segs[:k0]:
@@ -443,63 +459,71 @@ def rank_program(g, core, T, topo):
         tc(v("HL"), r)
         tc(v("P0"), at(v(F, 0, W), v("HL")))
         tc(v("H16"), v("H"))
-        tc(v("HW12"), r)
+        act(v("HW12"), r)
         act(v("XR", 0, 1536), at(v("X"), v("H16", 0, 96)))
         act(v("XR", 1536, 3072), at(v("X"), v("H16", 96, 192)))
         r = narrow(v("P0"), L)
         tc(v("P0L"), r)
-        tc(v("P0W"), r)
+        act(v("P0W"), r)
         tc(v("S0"), at(tab, v("P0L")))
         tc(v("P1"), at(v(F, 0, W), v("P0L")))
         tt(v("EQ0"), v("S0"), v("H"), eq)
         ts(v("EM0"), v("S0"), float(M), eq)
         mm(v("k6", 0, L), v("ONESB"), v("EQ0"), True, False)
         mm(v("k6", 0, L), v("ONESB"), v("EM0"), False, True)
+        W0, WD = v("k6", 256, 448), v("k7", 256, 448)
+        mm(W0, v("IDH"), v("S0"), True, False)
+        mm(W0, v("IDK"), v("EQ0"), False, True)
+        mm(WD, v("NIDH"), v("S0"), True, False)
+        mm(WD, v("NIDK"), v("EQ0"), False, False)
         r = narrow(v("P1"), L)
         tc(v("P1L"), r)
         tc(v("S1"), at(tab, v("P1L")))
-        ts(v("k5", 128, 320), v("EQ0"), float(BK), mul)
-        tt(v("W0"), v("k5", 128, 320), v("S0"), add)
+        mm(WD, v("IDH"), v("S1"), False, False)
+        ts(v("UR"), v("k6", 0, L), 16.0, ge)
         tt(v("EQ1"), v("S1"), v("P0"), eq)
-        ts(v("k5", 128, 320), v("EQ1"), float(BK), mul)
-        tt(v("k4", 0, L), v("k5", 128, 320), v("S1"), add)
-        tt(v("WD"), v("k4", 0, L), v("W0"), sub)
-        ts(v("k5", 320, 512), v("k6", 0, L), 16.0, ge)
-        tt(v("k4", 0, L), v("WD"), v("k5", 320, 512), mul)
-        tt(v("SA"), v("k4", 0, L), v("W0"), add)
+        mm(WD, v("IDK"), v("EQ1"), False, True)
+        tt(v("UD"), WD, v("UR"), mul)
+        tt(v("SA"), W0, v("UD"), add)
         tc(v("SA16"), v("SA"))
         yield
 
     def own_flags(t):
         act(v("XL"), at(v("X"), v("HL")))
-        r = narrow(v("k5", 320, 512), L)
+        for r in range(16):
+            mm(v("k6", 448, 460), v("SEL", 128 * r, 128 * (r + 1)), v("UR", r, L, 16), r == 0, r == 15)
         if t < 3:
             act(v("HG"), at(v("GH"), v("HL")))
-        tc(v("U2", 0, 12), r)
-        tc(v("U2", 12, 24), r)
+        act(v("U2", 0, 12), v("k6", 448, 460), scale=1.0 / 256)
+        act(v("U2", 12, 24), v("k6", 448, 460), scale=1.0 / 256)
         ts(v("ND"), v("P0W"), 64.0, lt)
         tt(v("ND"), v("ND"), v("U2", 0, 12), mul)
         ts(v("ND"), v("ND"), -1.0, mul, 1.0, add)
-        tc(v("Z4", 0, 12), v("HW12"))
+        act(v("Z4", 0, 12), v("HW12"))
         if t < 3:
             ts(v("LOF"), v("HW12"), float(M), ne)
             fill(v("ms%d" % t, 0, 384), 0.0)
             fill(v("HGS%d" % t, 0, 384), 0.0)
         yield
 
-    def down(tag, nq, idx, son, offl, xr, u, u0, lst, keep=None, cuts=2):
+    def down(tag, nq, idx, son, offl, xr, u, u0, lst, keep=None):
         n = nq * 16
-        kb, vb = {"A1": ("k0", "k3"), "A2": ("k1", "k4"), "AB": ("k2", "k5")}[tag]
-        c = n // cuts
-        for j in range(cuts):
-            a, b = j * c, (j + 1) * c
-            ux = v(u, u0 + 16 * a, u0 + 16 * b)
-            tt(ux, at(v("X"), v(idx, offl + a, offl + b)), v(xr, u0 + 16 * a, u0 + 16 * b), sub)
-            act(ux, ux, AF.Abs)
-            for s in range(16):
-                mm(v(kb, a, b), v("SEL", 128 * s, 128 * (s + 1)), v(u, u0 + 16 * a + s, u0 + 16 * b, 16), s == 0, False)
-            mm(v(kb, a, b), v("SLR", p=(0, 1)), v("ONES", 0, c, p=(0, 1)), False, True)
-        SP, KP = v(vb, 0, n), v(vb, n, 2 * n) if tag == "AB" else v(vb, 128, 128 + n)
+        kb, vb, vo = {"A0": ("k0", "k3", 0), "A1": ("k1", "k3", 128), "A2": ("k7", "k4", 0), "AB": ("k2", "k5", 0)}[tag]
+        nv = NV[tag]
+        if nv < n:
+            us, dif = v(u, u0 + 16 * nv, u0 + 16 * n), v(kb, 128, 128 + 16 * (n - nv))
+            act(us, at(v("X"), v(idx, offl + nv, offl + n)))
+            mm(dif, v("NIDB"), v(xr, u0 + 16 * nv, u0 + 16 * n), True, False)
+            mm(dif, v("IDB"), us, False, True)
+        ux = v(u, u0, u0 + 16 * nv)
+        tt(ux, at(v("X"), v(idx, offl, offl + nv)), v(xr, u0, u0 + 16 * nv), sub)
+        if nv < n:
+            act(us, dif, AF.Abs)
+        act(ux, ux, AF.Abs)
+        for s in range(16):
+            mm(v(kb, 0, n), v("SEL", 128 * s, 128 * (s + 1)), v(u, u0 + s, u0 + 16 * n, 16), s == 0, False)
+        mm(v(kb, 0, n), v("SLR", p=(0, 1)), v("ONES", 0, n, p=(0, 1)), False, True)
+        SP, KP = v(vb, vo, vo + n), v(vb, vo + n, vo + 2 * n)
         turn(SP, son)
         turn(KP, v(kb, 0, n))
         im, ni, zz, rr = [v(x + tag, 0, n) for x in ("IM", "NI", "ZZ", "RR")]
@@ -511,23 +535,23 @@ def rank_program(g, core, T, topo):
         scan(rr, ni, zz, mul, add)
         for e in range(2):
             for y in range(2):
-                mm(v(kb, 288 + e, 288 + nq, 2), v("SW", 128 * (2 * e + y), 128 * (2 * e + y + 1)), v("RR" + tag, 15 + 16 * y, n, 32), y == 0, y == 1)
-        lst(v(kb, 288, 288 + nq))
+                mm(v(kb, 64 + e, 64 + nq, 2), v("SWH", 128 * (2 * e + y), 128 * (2 * e + y + 1)), v("RR" + tag, 15 + 16 * y, n, 32), y == 0, y == 1)
+        lst(v(kb, 64, 64 + nq))
 
     def own(h):
-        tag, o, lo = ("A1", 0, 0) if h == 0 else ("A2", 6, 96)
+        tag, o, lo = "A%d" % h, 4 * h, 64 * h
 
         def after(step, name):
             def f(x):
                 if step < 2:
-                    tc(v(name, o, o + 6), x)
-                act(v("WALL", 12 * step + o, 12 * step + o + 6), x)
+                    tc(v(name, o, o + 4), x)
+                act(v("WALL", 12 * step + o, 12 * step + o + 4), x)
             return f
-        down(tag, 6, "SA16", v("SA", lo, lo + 96), lo, "XR", "UA", 1536 * h, after(0, "LA"))
+        down(tag, 4, "SA16", v("SA", lo, lo + 64), lo, "XR", "UA", 16 * lo, after(0, "LA"))
         for step, prev, name in ((1, "LA", "LB"), (2, "LB", "")):
-            tc(v("S16A", lo, lo + 96), at(v("SN"), v(prev, o, o + 6)))
-            act(v("SF" + tag), at(v("SN"), v(prev, o, o + 6)))
-            down(tag, 6, "S16A", v("SF" + tag), lo, "XR", "UA", 1536 * h, after(step, name), keep=192 * (step - 1) + lo)
+            tc(v("S16A", lo, lo + 64), at(v("SN"), v(prev, o, o + 4)))
+            act(v("SF" + tag), at(v("SN"), v(prev, o, o + 4)))
+            down(tag, 4, "S16A", v("SF" + tag), lo, "XR", "UA", 16 * lo, after(step, name), keep=192 * (step - 1) + lo)
         yield
 
     def arrivals(t):
@@ -549,7 +573,7 @@ def rank_program(g, core, T, topo):
                     tc(v("BL"), x)
                 if e:
                     act(v("LB3", 4 * (e - 1), 4 * e), x)
-            down("AB", 4, "S16B", v("SFAB"), 0, "XRB", "UB", 0, f, cuts=1)
+            down("AB", 4, "S16B", v("SFAB"), 0, "XRB", "UB", 0, f)
         ts(v("LBT"), v("LB3"), -float(M), add)
         tt(v("LB3"), v("LBT"), v("GENM"), mul)
         tt(v("LBT", 0, 4), v("LB3", 0, 4), v("LB3", 4, 8), add)
@@ -572,7 +596,7 @@ def rank_program(g, core, T, topo):
             else:
                 send(g, topo, core, mid, T["b" + k][:], src[3], T.sem["x" + k], T.sem.lo)
             sent[0] += NENG
-            when[("a" + k, NENG)] = free["g"] + 6.0
+            when[("a" + k, NENG)] = free["g"] + 10.0
         emit("g", call, [src], [], 1.0)
 
     def found(t):
@@ -583,8 +607,8 @@ def rank_program(g, core, T, topo):
         tt(v("FND", 0, 12), v("YT", 0, 12), v("ND"), mul)
         tt(v("FND", 12, 24), v("YT", 0, 12), v("ND"), mul)
         if t < 3:
-            tt(v("LO"), v("LOF"), v("FND", 0, 12), sub)
             tt(v("LOF"), v("LOF"), v("FND", 0, 12), sub)
+            act(v("LO"), v("LOF"))
             mm(v("k0", 256, 268), v("ONESB"), v("LO"), True, True)
             mm(v("k0", 272, 284), v("TRMO"), v("LO"), True, True)
         yield
@@ -592,14 +616,13 @@ def rank_program(g, core, T, topo):
     def adopt(t):
         ts(v("D1"), v("YS"), 1.0, add)
         tc(v("YL"), v("YS", 0, 12))
-        tt(v("YT"), v("D1"), v("FND"), mul)
+        tt(v("BS0", 0, 384, 16), v("D1"), v("FND"), mul)
         tc(v("SL"), v("YS", 12, 24))
-        ts(v("BS0", 0, 384, 16), v("YT"), -1.0, add)
         scan(v("SCB"), v("RS0"), v("BS0"), mul, add)
         tt(v("DX", 0, L), v("SCB", 0, L), DIAGB, mul)
-        mm(v("k7", 0, L), v("ONESF"), v("DX", 0, L), True, True)
+        mm(v("k7", 0, L), v("ONESH"), v("DX", 0, L), True, True)
         tt(v("DX", L, 384), v("SCB", L, 384), DIAGB, mul)
-        mm(v("k7", L, 384), v("ONESF"), v("DX", L, 384), True, True)
+        mm(v("k7", L, 384), v("ONESH"), v("DX", L, 384), True, True)
         tc(v("SY"), at(v("SN"), v("YL")))
         act(v("Z4", 12, 24), v("YS", 12, 24))
         act(v("Z4", 24, 36), v("YS", 0, 12))
@@ -607,7 +630,14 @@ def rank_program(g, core, T, topo):
         ts(v("EMY"), v("SY"), float(M), ne)
         mm(v("k1", 0, L), v("ONESB"), v("EMY"), True, True)
         tt(v("Z5"), v("Z4"), v("TR4"), sub)
-        tc(v("YR16"), v("k7", 0, 384))
+        act(v("SROW"), v("k7", L, 384))
+        o = 0
+        for q in range(11):
+            n = (11 - q) * 16
+            act(v("EZ", o, o + n), v("SROW", L - n, L), AF.Abs, bias=v("BS0", L + 16 * q, L + 16 * q + 1), scale=-1.0)
+            o += n
+        act(v("EC"), v("EZ"), AF.Relu, bias=1.0, scale=-1.0)
+        tc(v("YR16", 0, L), v("k7", 0, L))
         tt(v("k5", 128, 512), v("SCB"), v("k7", 0, 384), eq)
         tt(v("EDM"), v("k5", 128, 512), v("LTM"), mul)
         mm(v("k6", 0, L), v("ONESB"), v("EDM", 0, L), True, False)
@@ -615,10 +645,14 @@ def rank_program(g, core, T, topo):
         o = 0
         for q in range(11):
             n = (11 - q) * 16
-            for z in range(2):
-                ts(v("EE", o, o + n), v("YR16", L * z + L - n, L * z + L), v("BS0", L * z + 16 * q, L * z + 16 * q + 1), eq)
-                mm(v("k6", L - n, L), v("ONESB"), v("EE", o, o + n), False, q == 10 and z == 1)
-                o += n
+            ts(v("EE", o, o + n), v("YR16", L - n, L), v("BS0", 16 * q, 16 * q + 1), eq)
+            mm(v("k6", L - n, L), v("ONESB"), v("EE", o, o + n), False, False)
+            o += n
+        o = 0
+        for q in range(11):
+            n = (11 - q) * 16
+            mm(v("k6", L - n, L), v("ONESB"), v("EC", o, o + n), False, q == 10)
+            o += n
         tt(v("SR"), v("D15"), v("k1", 0, L), lt)
         scan(v("SRS"), v("RS0", 0, L), v("SR"), mul, add)
         tt(v("FR"), v("DIAG"), v("k6", 0, L), gt)
@@ -735,21 +769,22 @@ def rank_program(g, core, T, topo):
         st["lanes1" + p] = (1, ["returns" + last] if t else [], record(lanes1(t)))
         st["lanes2" + p] = (1, ["lanes1" + p] + (["rest" + last, "guests" + last, "sending" + last] if t else ["late"]), record(lanes2(t)))
         if t:
-            st["arrivals" + p] = (0, ["rest" + last, "guests" + last, "returns" + last], record(arrivals(t)))
+            st["arrivals" + p] = (2, ["rest" + last, "guests" + last, "returns" + last], record(arrivals(t)))
         else:
             st["last"] = (6, ["lanes2" + p], record(constants_last()))
         st["own0" + p] = (2, ["lanes2" + p], record(own(0)))
         st["own1" + p] = (3, ["lanes2" + p], record(own(1)))
+        st["own2" + p] = (4, ["lanes2" + p], record(own(2)))
         st["flags" + p] = (4, ["lanes2" + p, "last"], record(own_flags(t)))
-        st["found" + p] = (1, ["own0" + p, "own1" + p, "flags" + p], record(found(t)))
+        st["found" + p] = (1, ["own0" + p, "own1" + p, "own2" + p, "flags" + p], record(found(t)))
         st["adopt" + p] = (1, ["found" + p], record(adopt(t)))
         over = ["adopt" + p] + (["arrivals" + p] if t else [])
         if t < 3:
             st["slots" + p] = (2, ["found" + p] + (["arrivals" + p] if t else []), record(slots(t)))
-            st["sending" + p] = (3, ["found" + p], record(sending(t)))
+            st["sending" + p] = (0, ["found" + p], record(sending(t)))
             st["sons" + p] = (1, over + ["slots" + p], record(change_sons(t)))
             st["noted" + p] = (5, ["sending" + p], record(note_sent(t)))
-        st["returns" + p] = (2, (["sons" + p] if t < 3 else over) + (["noted" + last] if t else []), record(returns(t)) if t else [])
+        st["returns" + p] = (4, (["sons" + p] if t < 3 else over) + (["noted" + last] if t else []), record(returns(t)) if t else [])
         st["rest" + p] = (4, over, record(change_rest(t)))
         st["guests" + p] = (4, ["rest" + p, "returns" + p], record(guests(t)))
     merge(st)

from concourse.mybir import AluOpType as OP, ActivationFunctionType as AF

M, W, L, S, T_, Q = 1744, 1952, 192, 64, 4, 560
BK = 2176
WT = BK + W + 32
HWN = W + L
TB = W
BIG = 512.0
SW_ = 68
NENG = 8
NV = {"A0": 48, "A1": 48, "A2": 64, "AB": 48}

SCRATCH = {}
PLACE = {}
HALF = set()
BANKS = set("k%d" % i for i in range(8))
POOL = {"float32": ["poolf", 0], "float16": ["poole", 0], "bfloat16": ["poolh", 0], "int32": ["pooli", 0], "uint16": ["poolu", 0]}


def _b(kind, dtype, **kw):
    for n, w in kw.items():
        if dtype in ("bfloat16", "uint16", "float16"):
            HALF.add(n)
        if kind == "psum" or n[:2] in ("ms", "bs", "ls", "mr", "br", "lr"):
            SCRATCH[n] = (kind, [128, w], dtype)
        else:
            p = POOL[dtype]
            PLACE[n] = (p[0], p[1], w)
            p[1] += (w + 15) // 16 * 16
            SCRATCH[p[0]] = (kind, [128, p[1]], dtype)


_b("sbuf", "float32", SN=WT, F1=W + L, F2=W + L, GH=W, H=L, TMP=L, RW=L, P0=L, P1=L, SA=L, HG=L, RMOD=384, DIAG=L, LTM=384, RS0=384, RST=96, D15=L, OF=128, I3=384, SW=512,
   R16=1, PBF=2, M0=1, E0=1, TRL=12, TR4=48, COLC=64, ZER=122, HW12=12, P0W=12, U2=24, ND=12, WALL=36, KALL=24, D1=24, YS=24, KF=12, AW=12, FND=24, YT=24, BS0=384, SCB=384,
   BSA=L, FR=L, FRS=L, SR=L, SRS=L, FL4=48, Z4=48, Z5=48, SY=L, DD=L, VH=L, VY=L, XG=L, LOF=12,
   CS=12, DA=12, DB=12, RT=S, RTS=S, RTB=S, RTSB=S, FDW=4, RZ=4, RV=S, RV2=S, RVB=S, RV2B=S, FD=S, GENM=12, LB3=12, LBT=12,
   LFF=128, LG=128, G2K=128, MTC=8, MKEEP=384)
for _n in ("A0", "A1", "A2", "AB"):
    _b("sbuf", "float32", **{"SF" + _n: 64, "MM" + _n: 64, "IM" + _n: 64, "NI" + _n: 64, "ZZ" + _n: 64})
    _b("sbuf", "float16", **{"RR" + _n: 64})
_b("sbuf", "float16", SWH=512, ONESH=128, DX=384, FGF=M, LF=128, IDH=128, NIDH=128, S0=L, S1=L)
_b("sbuf", "bfloat16", IDK=128, NIDK=128, UR=L, EC=1056, EZ=1056)
_b("sbuf", "float32", UD=L, SROW=L)
SCRATCH["gnd"] = ("dram", [8, Q * 3 + W], "int32")
_b("sbuf", "float32", HWIN=HWN, D=W, R122=1, POS=122, GTH=488, NOK=122, C1=122)
_b("sbuf", "bfloat16", NINC=122, IDB=128, NIDB=128)
_b("sbuf", "int32", GTI=488, PAD=208)
_b("sbuf", "uint16", OFF16=122)
_b("sbuf", "bfloat16", X=WT, ANE=W, SEL=2048, WSEL=2048, ONES=128, ONESB=128, TRI=128, TRMO=128, SLR=128, XL=L, XR=3072,
   XRB=1024, UA=3072, UB=1024, EQ0=L, EM0=L, EQ1=L, EDM=384, EE=2112, EMY=L, AX=L, LO=12, WC=1, TMPB=128,
   FGB=M, LGB=128, VH8=W, VL8=W)
_b("sbuf", "int32", SNI=M, FGI=M, PI=1, PI2=1, LKI=64, KI=12, KI2=12, HI4=4, HI4B=4, HIR=S, HIR2=S,
   CI=4, CI2=4, XI=L)
_b("sbuf", "uint16", H16=L, HL=12, P0L=12, P1L=12, SA16=L, S16B=64, S16A=L, LA=12, LB=12, LK=64, BL=4,
   YR16=384, YL=12, SL=12, L4=48, LO16=12, RL16=4, BF16=4)
_b("psum", "float32", k0=512, k1=512, k2=512, k3=512, k4=512, k5=512, k6=512, k7=512)
for _t in range(3):
    _b("sbuf", "bfloat16", **{"ms%d" % _t: 384, "bs%d" % _t: SW_, "ls%d" % _t: SW_, "mr%d" % (_t + 1): S, "br%d" % (_t + 1): S, "lr%d" % (_t + 1): S})
    _b("sbuf", "float32", **{"HGS%d" % _t: 384, "HROW%d" % _t: S, "GHN%d" % _t: S, "HSW%d" % _t: 4})
    _b("sbuf", "uint16", **{"HS%d" % _t: 4})

MSGS = [("s", 0), ("r", 1), ("s", 1), ("r", 2), ("s", 2), ("r", 3)]
SEMAPHORES = ["qv", "qs", "qt", "qg", "lo"] + ["d%d" % i for i in range(24)] + ["x%s%d" % m for m in MSGS] + ["a%s%d" % m for m in MSGS]


def goal(T, rank, kind, t):
    return T.cores[(rank + 1 + t) % 4] if kind == "s" else T.cores[(rank - t) % 4]


def via(topo, src, dst):
    if topo.may_write(src, dst):
        return None
    c = [k for k in topo.cores_of(src) if k != src and topo.may_write(k, dst)]
    near = [k for k in c if topo.die(k) == topo.die(src)]
    return (near + c)[0]


def send(g, topo, src, dst, out, in_, rsem, lsem):
    rid, pid = topo.addr(dst, src)
    mask = sum(1 << e for e in topo.engines(src, dst)[:NENG])
    g.remote_dma(out, in_, rsem, lsem, pid, rid, mask)


def hand_on(g, core, T, topo):
    n = 0
    for kind, t in MSGS:
        for r in range(len(T.cores)):
            dst = goal(T, r, kind, t)
            if via(topo, T.cores[r], dst) == core:
                k = "%s%d" % (kind, t)
                g.wait_ge(T.sem["x" + k], NENG)
                send(g, topo, core, dst, T["l" + k][:], T["b" + k][:], T.sem["a" + k], T.sem.lo)
                n += NENG
    if n:
        g.wait_ge(T.sem.lo, n)


def rank_program(g, core, T, topo):
    rank = T.rank_of(core)
    if rank is None:
        hand_on(g, core, T, topo)
        return

    queue = {"v": g.vector, "s": g.scalar, "t": g.tensor, "g": g, "y": g.sync}
    count = {"qv": 0, "qs": 0, "qt": 0, "qg": 0}
    known = {e: {} for e in queue}
    clock = {}
    wr, rd = {}, {}
    dsem = [0]
    total = {}
    WAKE, CY = 0.1, 0.00083
    free = {e: 0.0 for e in queue}
    when = {}
    tape = [None]

    def deps(e, reads, writes):
        w = {}

        def want(sem, val):
            if known[e].get(sem, 0) < val and w.get(sem, 0) < val:
                w[sem] = val
        for isw, lst in ((0, reads), (1, writes)):
            for n, lo, hi in lst:
                ps = n in BANKS
                for lo2, hi2, e2, sem, val in wr.get(n, ()):
                    if ps and e2 != e or lo < hi2 and lo2 < hi:
                        if not (e == "t" and e2 == "t" and ps):
                            want(sem, val)
                if isw or ps:
                    for (e2, lo2, hi2), (sem, val) in rd.get(n, {}).items():
                        if ps and e2 != e or (isw and lo < hi2 and lo2 < hi):
                            want(sem, val)
        return w

    def need(e, reads, writes):
        w = deps(e, reads, writes)
        for sem in w:
            free[e] = max(free[e], when.get((sem, w[sem]), 0) + WAKE)
        for sem in sorted(w):
            if known[e].get(sem, 0) >= w[sem]:
                continue
            queue[e].wait_ge(T.sem[sem], w[sem])
            known[e][sem] = w[sem]
            for s2, v2 in clock.get((sem, w[sem]), {}).items():
                if known[e].get(s2, 0) < v2:
                    known[e][s2] = v2

    def note(e, sem, val, reads, writes):
        c = dict(known[e])
        if sem[0] == "q":
            for s2, v2 in clock.get((sem, val - 1), {}).items():
                if c.get(s2, 0) < v2:
                    c[s2] = v2
        c[sem] = val
        clock[(sem, val)] = c
        total[sem] = max(total.get(sem, 0), val)
        for n, lo, hi in writes:
            wr[n] = [x for x in wr.get(n, []) if not (lo <= x[0] and x[1] <= hi)] + [(lo, hi, e, sem, val)]
            rd[n] = {k: x for k, x in rd.get(n, {}).items() if not (lo <= k[1] and k[2] <= hi)}
        for n, lo, hi in reads:
            rd.setdefault(n, {})[(e, lo, hi)] = (sem, val)

    def flat(xs):
        r = []
        for x in xs:
            if x is not None and not isinstance(x, (int, float)):
                r += [x[0:3]] if len(x) == 4 else [x[0][0:3], x[1][0:3]]
        return r

    def ap(x):
        return x if x is None or isinstance(x, (int, float)) else x[3] if len(x) == 4 else x[2]

    def emit(e, call, reads, writes, us):
        if tape[0] is not None:
            tape[0].append((e, call, flat(reads), flat(writes), us))
        else:
            issue(e, call, flat(reads), flat(writes), us)

    def issue(e, call, reads, writes, us):
        need(e, reads, writes)
        free[e] += us
        if writes:
            sem = "q" + e
            count[sem] += 1
            call().then_inc(T.sem[sem], 1)
            when[(sem, count[sem])] = free[e]
            note(e, sem, count[sem], reads, writes)
        else:
            call()

    def record(gen):
        tape[0] = []
        for _ in gen:
            pass
        r = tape[0]
        tape[0] = None
        return r

    def merge(streams):
        pos = {n: 0 for n in streams}
        done = set()
        while len(done) < len(streams):
            best = None
            for n in streams:
                if n in done or any(p not in done for p in streams[n][1]):
                    continue
                if pos[n] == len(streams[n][2]):
                    done.add(n)
                    best = None
                    break
                e, call, reads, writes, us = streams[n][2][pos[n]]
                st = free[e]
                w = deps(e, reads, writes)
                for sem in w:
                    st = max(st, when.get((sem, w[sem]), 0) + WAKE)
                key = (round(st / 0.04), streams[n][0], st)
                if best is None or key < best[0]:
                    best = (key, n)
            if best is not None:
                n = best[1]
                issue(*streams[n][2][pos[n]])
                pos[n] += 1

    def size(x):
        return x[3].shape[1] if len(x) == 4 else 16 * x[1][3].shape[1]

    def two(*xs):
        return all(len(x) == 4 and (x[0] in HALF) for x in xs)

    def dma(e, out, in_):
        reads, writes = flat([in_]), flat([out])
        need(e, reads, writes)
        sem = "d%d" % dsem[0]
        dsem[0] += 1
        queue[e].dma_start(ap(out), ap(in_)).then_inc(T.sem[sem], 16)
        free[e] += 0.1
        when[(sem, 16)] = free[e] + (6.0 if out[0] in ("SNI", "X") else 3.0)
        note(e, sem, 16, reads, writes)

    def v(name, lo=0, hi=None, st=1, p=None):
        buf, o, w = PLACE[name] if name in PLACE else (name, 0, SCRATCH[name][1][1])
        t = T[buf]
        if hi is None:
            hi = w
        ps = slice(None) if p is None else slice(*p)
        return (name, lo, hi, t[ps, o + lo:o + hi] if st == 1 else t[ps, o + lo:o + hi:st])

    def at(win, off):
        return (win, off, win[3].indirect(off[3]))

    def tc(out, in_):
        sc, ga = len(out) == 3, len(in_) == 3
        emit("v", lambda: g.vector.tensor_copy(ap(out), ap(in_)), [in_] + ([out[1]] if sc else []), [out[0] if sc else out],
             0.05 + 3.8 * CY * size(out) if sc else 0.05 + 1.5 * CY * size(in_) if ga else CY * max(64, size(out) * (0.5 if two(out, in_) else 1)))

    def tt(out, a, b, op):
        emit("v", lambda: g.vector.tensor_tensor(ap(out), ap(a), ap(b), op), [a, b], [out],
             0.05 + 1.5 * CY * size(a) if len(a) == 3 else CY * max(64, size(out) * (1 if a[0] in BANKS or b[0] in BANKS else 2)))

    def ts(out, a, s1, op0, s2=None, op1=None):
        us = CY * max(64, size(out) * (0.5 if two(out, a) else 1))
        if op1 is None:
            emit("v", lambda: g.vector.tensor_scalar(ap(out), ap(a), ap(s1), None, op0), [a, s1], [out], us)
        else:
            emit("v", lambda: g.vector.tensor_scalar(ap(out), ap(a), ap(s1), ap(s2), op0, op1), [a, s1, s2], [out], us)

    def scan(out, d0, d1, op0, op1, init=0.0):
        emit("v", lambda: g.vector.tensor_tensor_scan(ap(out), ap(d0), ap(d1), init, op0, op1), [d0, d1], [out], CY * max(64, size(out)))

    def turn(out, in_):
        emit("v", lambda: g.vector.transpose(ap(out), ap(in_)), [in_], [out], CY * max(64, size(out)))

    def fill(out, c):
        emit("v", lambda: g.vector.memset(ap(out), c), [], [out], CY * max(64, size(out)))

    def act(out, in_, func=AF.Copy, bias=0.0, scale=1.0):
        us = 0.065 + 1.5 * CY * size(out) if len(in_) == 3 else CY * max(64, size(out))
        if bias != 0.0 or scale != 1.0:
            emit("s", lambda: g.scalar.activation(ap(out), ap(in_), func, bias=ap(bias), scale=scale), [in_, bias], [out], us)
        else:
            emit("s", lambda: g.scalar.activation(ap(out), ap(in_), func), [in_], [out], us)

    def mm(out, lhsT, rhs, start, stop):
        emit("t", lambda: g.tensor.matmul(ap(out), ap(lhsT), ap(rhs), start, stop), [lhsT, rhs], [out], CY * max(64, size(out)) * (1 if two(lhsT) else 4))

    def iota(out, pattern, base, cm, small=False):
        us = 0.15 + 2 * CY * size(out)
        if small:
            emit("g", lambda: g.iota(ap(out), pattern, base, cm, allow_small_or_imprecise_dtypes=True), [], [out], us)
        else:
            emit("g", lambda: g.iota(ap(out), pattern, base, cm), [], [out], us)

    def pick(out, in_, pattern, op, base, cm):
        emit("g", lambda: g.affine_select(ap(out), ap(in_), pattern, op, 0.0, base, cm), [in_], [out], 0.17 + 2 * CY * size(out))

    add, sub, mul, eq, ne = OP.add, OP.subtract, OP.mult, OP.is_equal, OP.not_equal
    ge, gt, lt = OP.is_ge, OP.is_gt, OP.is_lt

    half = M // 2
    dma("s", ("gnd", 0, M, T.gnd[:, 0:M]), ("gn", 0, M, T.gn[:]))
    dma("s", ("gnd", W, Q * 3 + W, T.gnd[:, W:Q * 3 + W]), ("gn", 0, Q * 3, T.gn[:, 0:Q * 3]))
    dma("y", v("SNI", 0, half), ("sn", 0, half, T.sn[:, 0:half]))
    dma("y", v("SNI", half, M), ("sn", half, M, T.sn[:, half:M]))
    dma("s", v("FGI", 0, M, p=(0, 8)), ("fa", 0, M, T.fa[:]))
    dma("s", v("FGI", 0, M, p=(8, 16)), ("gn", 0, M, T.gn[:]))
    dma("y", v("X", 0, M), ("x", 0, M, T.x[:]))
    dma("y", v("WC"), ("w", 0, 1, T.w[:]))

    fill(v("PAD", 0, 16), 0)
    fill(v("PAD", 16, 208), 2)
    dma("s", ("gnd", M, W, T.gnd[:, M:W]), v("PAD", p=(0, 8)))
    for t in range(T_):
        dma("s", v("GTI", 122 * t, 122 * (t + 1)), ("gnd", Q * t, Q * t + W, T.gnd[:, Q * t:Q * t + W]))

    iota(v("PI"), [[1, 1]], 0, 1)
    fill(v("ONES"), 1.0)
    pick(v("TMPB"), v("ONES"), [[-16, 8], [0, 16]], ge, 0, 1)
    pick(v("ONESB"), v("TMPB"), [[16, 8], [0, 16]], ge, 15, -1)
    pick(v("TRI"), v("ONESB"), [[1, 128]], ge, -1, -1)
    iota(v("RMOD"), [[0, 24], [1, 16]], 0, 0, True)
    iota(v("POS"), [[1, 122]], 0, 0, True)
    iota(v("D"), [[1, 122], [122, 16]], 0, 0, True)
    ts(v("PI2"), v("PI"), 15, OP.bitwise_and)
    tc(v("R16"), v("PI2"))
    ts(v("PI2"), v("PI"), 4, OP.logical_shift_right, 1, OP.bitwise_and)
    tc(v("PBF", 1, 2), v("PI2"))
    ts(v("PBF", 0, 1), v("PBF", 1, 2), -1.0, mul, 1.0, add)
    R16 = v("R16")
    POSB, CQB, DIAGB = v("k4", 256, 378), v("k4", 384, 506), v("k3", 256, 448)
    ts(v("R122"), R16, 122.0, mul)
    ts(POSB, v("POS"), v("R122"), add)
    ts(CQB, POSB, -1.0, mul, float(HWN), add)
    fill(v("ZER"), 0.0)
    fill(v("SEL"), 0.0)
    for s in range(16):
        ts(v("SEL", s * 128 + s, (s + 1) * 128, 16), v("ONESB", s, 128, 16), 16.0, mul)
    fill(v("SN", M, 1760), float(M))
    fill(v("SN", 1760, W), 0.0)
    fill(v("SN", W, WT), float(M))
    tc(v("SN", 0, half), v("SNI", 0, half))
    tc(v("SN", half, M), v("SNI", half, M))
    ts(v("GTH"), v("GTI"), 2, ge, -1.0, add)
    iota(v("SLR"), [[0, 8], [1, 16]], 0, 0, True)
    fill(v("OF"), 1.0)
    for i, base in enumerate((0, 16, -16)):
        pick(v("I3", 128 * i, 128 * (i + 1)), v("OF"), [[-1, 128]], eq, base, 1)
    fill(v("G2K"), 2048.0)
    pick(v("LG", p=(0, 16)), v("G2K", p=(0, 16)), [[1, 8], [0, 16]], eq, 8, -1)
    pick(v("LFF", p=(0, 16)), v("OF", p=(0, 16)), [[1, 8], [0, 16]], eq, 0, -1)
    iota(v("TRL"), [[16, 12]], L, 0, True)
    iota(v("TR4"), [[0, 4], [16, 12]], TB, 0, True)
    iota(v("LKI"), [[1, 64]], 0, 0)
    iota(v("COLC"), [[1, 64]], 1760, 0, True)
    iota(v("VH8", p=(0, 1)), [[8, W // 8], [0, 8]], 0, 0, True)
    iota(v("VL8", p=(0, 1)), [[0, W // 8], [1, 8]], 0, 0, True)

    def constants_late():
        tc(v("FGF", p=(0, 16)), v("FGI", p=(0, 16)))
        tc(v("LF", p=(0, 16)), v("LFF", p=(0, 16)))
        ts(v("DIAG"), v("RMOD", 0, L), R16, eq)
        ts(DIAGB, v("RMOD", 0, L), R16, eq)
        ts(v("RS0"), v("RMOD"), 0.0, ne)
        ts(v("RST"), v("RMOD", 0, 96), 0.0, eq, float(2 ** 20), mul)
        fill(v("F1", M, 1760), float(M))
        fill(v("F1", 1760, W + L), 0.0)
        fill(v("F2", M, 1760), float(M))
        fill(v("F2", 1760, W + L), 0.0)
        fill(v("GH", M, W), 0.0)
        fill(v("X", M, WT), BIG)
        fill(v("X", 1760, W), 0.0)
        w = M // 4
        for j in range(4):
            a, b = j * w, (j + 1) * w
            k = "k%d" % (2 * (j % 2))
            mm(v(k, 0, w), v("LF", p=(0, 16)), v("FGF", a, b, p=(0, 16)), True, True)
            act(v("F1", a, b), v(k, 0, w))
        for e in range(2):
            for y in range(2):
                i = 0 if e == y else 1 if y else 2
                ts(v("SW", 128 * (2 * e + y), 128 * (2 * e + y + 1)), v("I3", 128 * i, 128 * (i + 1)), v("PBF", e, e + 1), mul)
        tc(v("SWH"), v("SW"))
        act(v("IDB"), v("I3", 0, 128))
        act(v("NIDB"), v("I3", 0, 128), scale=-1.0)
        act(v("IDK"), v("I3", 0, 128), scale=float(BK))
        act(v("NIDK"), v("I3", 0, 128), scale=-float(BK))
        tc(v("IDH"), v("I3", 0, 128))
        ts(v("NIDH"), v("I3", 0, 128), -1.0, mul)
        ts(v("TRL"), v("TRL"), R16, add)
        ts(v("TR4"), v("TR4"), R16, add)
        yield

    def constants_last():
        tc(v("FGB", p=(0, 16)), v("FGI", p=(0, 16)))
        tc(v("LGB", p=(0, 16)), v("LG", p=(0, 16)))
        act(v("F2", 0, M), v("F1", 0, M))
        w = M // 4
        for j in range(4):
            a, b = j * w, (j + 1) * w
            k = "k2"
            mm(v(k, 0, w), v("LGB", p=(0, 16)), v("FGB", a, b, p=(0, 16)), True, False)
            mm(v(k, 0, w), v("ONES", p=(0, 1)), v("VH8", a, b, p=(0, 1)), False, False)
            mm(v(k, 0, w), v("ONES", p=(0, 1)), v("VL8", a, b, p=(0, 1)), False, True)
            act(v("GH", a, b), v(k, 0, w))
        ts(v("LTM"), v("RMOD"), R16, gt)
        ts(v("D15"), v("DIAG"), -998.5, mul, 1000.0, add)
        ts(v("M0"), R16, 0.0, eq)
        ts(v("E0"), R16, 0.0, ne, float(M + 1), mul)
        ts(v("E0"), v("E0"), -1.0, add)
        for t in range(1, 4):
            ts(v("MTC", t, t + 1), R16, float(t), eq)
            ts(v("MTC", 4 + t, 5 + t), R16, float(t), ne)
        tc(v("ONESH"), v("ONESB"))
        tt(v("TRMO"), v("TRI"), v("ONESB"), sub)
        ts(v("WSEL"), v("SEL"), v("WC"), mul, 0.0625, mul)
        fill(v("BS0"), 0.0)
        fill(v("BSA"), 0.0)
        tc(v("LK"), v("LKI"))
        yield

    def narrow(src, n, tmp="TMP", res="RW"):
        tt(v(tmp, 0, n), src, v("DIAG", 0, n) if src[0] in BANKS else v("k3", 256, 256 + n), mul)
        scan(v(res, 0, n), v("RS0", 0, n), v(tmp, 0, n), mul, add)
        return v(res, 15, n, 16)

    def lanes1(t):
        c = W // 4
        st = Q * t
        segs = [(a, a + c) for a in range(0, W, c)]
        k0 = st // c
        fill(v("HWIN", 0, L), float(M))
        for a, b in segs[k0:] + segs[:k0]:
            act(v("ANE", a, b), v("SN", a, b), AF.Abs, -float(M))
        for m in range(16):
            a = st + 122 * m
            parts = [(a, a + 122)] if a + 122 <= W or a >= W else [(a, W), (W, a + 122)]
            for x, y in parts:
                mm(v("k6", x - a, y - a), v("SEL", 128 * m, 128 * (m + 1)), v("ANE", x % W, x % W + y - x), m == 0, m == 15)
        tt(v("NOK"), v("k6", 0, 122), v("GTH", 122 * t, 122 * (t + 1)), gt)
        scan(v("NINC"), v("NOK"), v("ZER"), add, add)
        mm(v("k7", 0, 1), v("TRI"), v("NINC", 121, 122), True, True)
        tt(v("C1"), v("NOK"), CQB, mul)
        tt(v("k3", 0, 122), v("C1"), POSB, add)
        tt(v("C1"), v("k3", 0, 122), v("NINC"), sub)
        ts(v("OFF16"), v("C1"), v("k7", 0, 1), sub)
        tc(at(v("HWIN"), v("OFF16")), v("D"))
        if t < 3:
            iota(v("D"), [[1, 122], [122, 16]], Q * (t + 1), 0, True)
        yield

    def lanes2(t):
        if t:
            ts(v("k4", 0, L), v("HWIN", 0, L), float(W), ge, -float(W), mul)
            tt(v("H"), v("k4", 0, L), v("HWIN", 0, L), add)
        else:
            tc(v("H"), v("HWIN", 0, L))
        F = "F1" if t % 2 == 0 else "F2"
        tab = v("SN")
        r = narrow(v("H"), L)
        tc(v("HL"), r)
        tc(v("P0"), at(v(F, 0, W), v("HL")))
        tc(v("H16"), v("H"))
        act(v("HW12"), r)
        act(v("XR", 0, 1536), at(v("X"), v("H16", 0, 96)))
        act(v("XR", 1536, 3072), at(v("X"), v("H16", 96, 192)))
        r = narrow(v("P0"), L)
        tc(v("P0L"), r)
        act(v("P0W"), r)
        tc(v("S0"), at(tab, v("P0L")))
        tc(v("P1"), at(v(F, 0, W), v("P0L")))
        tt(v("EQ0"), v("S0"), v("H"), eq)
        ts(v("EM0"), v("S0"), float(M), eq)
        mm(v("k6", 0, L), v("ONESB"), v("EQ0"), True, False)
        mm(v("k6", 0, L), v("ONESB"), v("EM0"), False, True)
        W0, WD = v("k6", 256, 448), v("k7", 256, 448)
        mm(W0, v("IDH"), v("S0"), True, False)
        mm(W0, v("IDK"), v("EQ0"), False, True)
        mm(WD, v("NIDH"), v("S0"), True, False)
        mm(WD, v("NIDK"), v("EQ0"), False, False)
        r = narrow(v("P1"), L)
        tc(v("P1L"), r)
        tc(v("S1"), at(tab, v("P1L")))
        mm(WD, v("IDH"), v("S1"), False, False)
        ts(v("UR"), v("k6", 0, L), 16.0, ge)
        tt(v("EQ1"), v("S1"), v("P0"), eq)
        mm(WD, v("IDK"), v("EQ1"), False, True)
        tt(v("UD"), WD, v("UR"), mul)
        tt(v("SA"), W0, v("UD"), add)
        tc(v("SA16"), v("SA"))
        yield

    def own_flags(t):
        act(v("XL"), at(v("X"), v("HL")))
        for r in range(16):
            mm(v("k6", 448, 460), v("SEL", 128 * r, 128 * (r + 1)), v("UR", r, L, 16), r == 0, r == 15)
        if t < 3:
            act(v("HG"), at(v("GH"), v("HL")))
        act(v("U2", 0, 12), v("k6", 448, 460), scale=1.0 / 256)
        act(v("U2", 12, 24), v("k6", 448, 460), scale=1.0 / 256)
        ts(v("ND"), v("P0W"), 64.0, lt)
        tt(v("ND"), v("ND"), v("U2", 0, 12), mul)
        ts(v("ND"), v("ND"), -1.0, mul, 1.0, add)
        act(v("Z4", 0, 12), v("HW12"))
        if t < 3:
            ts(v("LOF"), v("HW12"), float(M), ne)
            fill(v("ms%d" % t, 0, 384), 0.0)
            fill(v("HGS%d" % t, 0, 384), 0.0)
        yield

    def down(tag, nq, idx, son, offl, xr, u, u0, lst, keep=None):
        n = nq * 16
        kb, vb, vo = {"A0": ("k0", "k3", 0), "A1": ("k1", "k3", 128), "A2": ("k7", "k4", 0), "AB": ("k2", "k5", 0)}[tag]
        nv = NV[tag]
        if nv < n:
            us, dif = v(u, u0 + 16 * nv, u0 + 16 * n), v(kb, 128, 128 + 16 * (n - nv))
            act(us, at(v("X"), v(idx, offl + nv, offl + n)))
            mm(dif, v("NIDB"), v(xr, u0 + 16 * nv, u0 + 16 * n), True, False)
            mm(dif, v("IDB"), us, False, True)
        ux = v(u, u0, u0 + 16 * nv)
        tt(ux, at(v("X"), v(idx, offl, offl + nv)), v(xr, u0, u0 + 16 * nv), sub)
        if nv < n:
            act(us, dif, AF.Abs)
        act(ux, ux, AF.Abs)
        for s in range(16):
            mm(v(kb, 0, n), v("SEL", 128 * s, 128 * (s + 1)), v(u, u0 + s, u0 + 16 * n, 16), s == 0, False)
        mm(v(kb, 0, n), v("SLR", p=(0, 1)), v("ONES", 0, n, p=(0, 1)), False, True)
        SP, KP = v(vb, vo, vo + n), v(vb, vo + n, vo + 2 * n)
        turn(SP, son)
        turn(KP, v(kb, 0, n))
        im, ni, zz, rr = [v(x + tag, 0, n) for x in ("IM", "NI", "ZZ", "RR")]
        mm_ = v("MM" + tag, 0, n) if keep is None else v("MKEEP", keep, keep + n)
        scan(mm_, v("RST", 0, n), KP, add, OP.min, float(2 ** 20))
        tt(im, mm_, KP, eq)
        tt(ni, mm_, KP, ne)
        tt(zz, im, SP, mul)
        scan(rr, ni, zz, mul, add)
        for e in range(2):
            for y in range(2):
                mm(v(kb, 64 + e, 64 + nq, 2), v("SWH", 128 * (2 * e + y), 128 * (2 * e + y + 1)), v("RR" + tag, 15 + 16 * y, n, 32), y == 0, y == 1)
        lst(v(kb, 64, 64 + nq))

    def own(h):
        tag, o, lo = "A%d" % h, 4 * h, 64 * h

        def after(step, name):
            def f(x):
                if step < 2:
                    tc(v(name, o, o + 4), x)
                act(v("WALL", 12 * step + o, 12 * step + o + 4), x)
            return f
        down(tag, 4, "SA16", v("SA", lo, lo + 64), lo, "XR", "UA", 16 * lo, after(0, "LA"))
        for step, prev, name in ((1, "LA", "LB"), (2, "LB", "")):
            tc(v("S16A", lo, lo + 64), at(v("SN"), v(prev, o, o + 4)))
            act(v("SF" + tag), at(v("SN"), v(prev, o, o + 4)))
            down(tag, 4, "S16A", v("SF" + tag), lo, "XR", "UA", 16 * lo, after(step, name), keep=192 * (step - 1) + lo)
        yield

    def arrivals(t):
        ls = "ls%d" % (t - 1)
        for r in range(16):
            mm(v("k2", 0, 4), v("WSEL", 128 * r, 128 * (r + 1)), v(ls, r, S, 16), r == 0, r == 15)
        act(v("XRB"), at(v(ls, 0, S), v("LK")))
        tc(v("CI"), v("k2", 0, 4))
        for d in range(3):
            ts(v("GENM", 4 * d, 4 * d + 4), v(ls, S, SW_), float(d + 2), eq)
        ts(v("CI2"), v("CI"), 63, OP.bitwise_and)
        tc(v("BL"), v("CI2"))
        for e in range(4):
            tc(v("S16B"), at(v("SN"), v("BL")))
            act(v("SFAB"), at(v("SN"), v("BL")))

            def f(x):
                if e < 3:
                    tc(v("BL"), x)
                if e:
                    act(v("LB3", 4 * (e - 1), 4 * e), x)
            down("AB", 4, "S16B", v("SFAB"), 0, "XRB", "UB", 0, f)
        ts(v("LBT"), v("LB3"), -float(M), add)
        tt(v("LB3"), v("LBT"), v("GENM"), mul)
        tt(v("LBT", 0, 4), v("LB3", 0, 4), v("LB3", 4, 8), add)
        tt(v("LBT", 4, 8), v("LBT", 0, 4), v("LB3", 8, 12), add)
        ts(v("BF16"), v("LBT", 4, 8), float(M), add)
        tc(v("mr%d" % t), at(v("X"), v("BF16")))
        ship("r", t, v("mr%d" % t))
        yield

    sent = [0]

    def ship(kind, t, src):
        k = "%s%d" % (kind, t)
        dst = goal(T, rank, kind, t)
        mid = via(topo, core, dst)

        def call():
            if mid is None:
                send(g, topo, core, dst, T["l" + k][:], src[3], T.sem["a" + k], T.sem.lo)
            else:
                send(g, topo, core, mid, T["b" + k][:], src[3], T.sem["x" + k], T.sem.lo)
            sent[0] += NENG
            when[("a" + k, NENG)] = free["g"] + 10.0
        emit("g", call, [src], [], 1.0)

    def found(t):
        tt(v("D1"), v("WALL", 12, 36), v("WALL", 0, 24), sub)
        tt(v("YT"), v("D1"), v("U2"), mul)
        tt(v("YS"), v("YT"), v("WALL", 0, 24), add)
        ts(v("YT", 0, 12), v("YS", 12, 24), float(M), ne)
        tt(v("FND", 0, 12), v("YT", 0, 12), v("ND"), mul)
        tt(v("FND", 12, 24), v("YT", 0, 12), v("ND"), mul)
        if t < 3:
            tt(v("LOF"), v("LOF"), v("FND", 0, 12), sub)
            act(v("LO"), v("LOF"))
            mm(v("k0", 256, 268), v("ONESB"), v("LO"), True, True)
            mm(v("k0", 272, 284), v("TRMO"), v("LO"), True, True)
        yield

    def adopt(t):
        ts(v("D1"), v("YS"), 1.0, add)
        tc(v("YL"), v("YS", 0, 12))
        tt(v("BS0", 0, 384, 16), v("D1"), v("FND"), mul)
        tc(v("SL"), v("YS", 12, 24))
        scan(v("SCB"), v("RS0"), v("BS0"), mul, add)
        tt(v("DX", 0, L), v("SCB", 0, L), DIAGB, mul)
        mm(v("k7", 0, L), v("ONESH"), v("DX", 0, L), True, True)
        tt(v("DX", L, 384), v("SCB", L, 384), DIAGB, mul)
        mm(v("k7", L, 384), v("ONESH"), v("DX", L, 384), True, True)
        tc(v("SY"), at(v("SN"), v("YL")))
        act(v("Z4", 12, 24), v("YS", 12, 24))
        act(v("Z4", 24, 36), v("YS", 0, 12))
        act(v("Z4", 36, 48), v("YS", 12, 24))
        ts(v("EMY"), v("SY"), float(M), ne)
        mm(v("k1", 0, L), v("ONESB"), v("EMY"), True, True)
        tt(v("Z5"), v("Z4"), v("TR4"), sub)
        act(v("SROW"), v("k7", L, 384))
        o = 0
        for q in range(11):
            n = (11 - q) * 16
            act(v("EZ", o, o + n), v("SROW", L - n, L), AF.Abs, bias=v("BS0", L + 16 * q, L + 16 * q + 1), scale=-1.0)
            o += n
        act(v("EC"), v("EZ"), AF.Relu, bias=1.0, scale=-1.0)
        tc(v("YR16", 0, L), v("k7", 0, L))
        tt(v("k5", 128, 512), v("SCB"), v("k7", 0, 384), eq)
        tt(v("EDM"), v("k5", 128, 512), v("LTM"), mul)
        mm(v("k6", 0, L), v("ONESB"), v("EDM", 0, L), True, False)
        mm(v("k6", 0, L), v("ONESB"), v("EDM", L, 384), False, False)
        o = 0
        for q in range(11):
            n = (11 - q) * 16
            ts(v("EE", o, o + n), v("YR16", L - n, L), v("BS0", 16 * q, 16 * q + 1), eq)
            mm(v("k6", L - n, L), v("ONESB"), v("EE", o, o + n), False, False)
            o += n
        o = 0
        for q in range(11):
            n = (11 - q) * 16
            mm(v("k6", L - n, L), v("ONESB"), v("EC", o, o + n), False, q == 10)
            o += n
        tt(v("SR"), v("D15"), v("k1", 0, L), lt)
        scan(v("SRS"), v("RS0", 0, L), v("SR"), mul, add)
        tt(v("FR"), v("DIAG"), v("k6", 0, L), gt)
        scan(v("FRS"), v("RS0", 0, L), v("FR"), mul, add)
        tt(v("FL4", 0, 12), v("FRS", 15, L, 16), v("FND", 0, 12), mul)
        tt(v("FL4", 12, 24), v("FRS", 15, L, 16), v("FND", 0, 12), mul)
        tt(v("FL4", 24, 36), v("SRS", 15, L, 16), v("FL4", 0, 12), mul)
        tt(v("FL4", 36, 48), v("SRS", 15, L, 16), v("FL4", 0, 12), mul)
        tt(v("Z4"), v("Z5"), v("FL4"), mul)
        tt(v("Z5"), v("Z4"), v("TR4"), add)
        tc(v("L4"), v("Z5"))
        yield

    def slots(t):
        for e in range(2):
            for y in range(2):
                mm(v("k2", 256 + e, 280, 2), v("SW", 128 * (2 * e + y), 128 * (2 * e + y + 1)), v("MKEEP", 15 + 16 * y, 384, 32), y == 0, y == 1)
        act(v("KALL"), v("k2", 256, 280))
        tt(v("KF"), v("KALL", 12, 24), v("KALL", 0, 12), sub)
        tt(v("AW"), v("KF"), v("U2", 0, 12), mul)
        tt(v("KF"), v("AW"), v("KALL", 0, 12), add)
        tc(v("KI"), v("KF"))
        ts(v("KI2"), v("KI"), 15, OP.bitwise_and)
        tc(v("BSA", 0, L, 16), v("KI2"))
        scan(v("k4", 0, L), v("RS0", 0, L), v("BSA"), mul, add)
        tt(v("AX"), v("k4", 0, L), v("DIAG"), mul)
        mm(v("k0", 0, L), v("ONESB"), v("AX"), True, True)
        yield

    def change_sons(t):
        ts(v("VH"), v("k7", L, 384), v("M0"), mul, v("E0"), add)
        ts(v("DD"), v("SY"), -1.0, mul, float(M), add)
        ts(v("k1", 0, L), v("k0", 0, L), R16, eq)
        tc(at(v("SN", 0, W + L), v("L4", 0, 12)), v("VH"))
        tt(v("k3", 0, L), v("DD"), v("k1", 0, L), mul)
        tt(v("VY"), v("k3", 0, L), v("SY"), add)
        tc(at(v("SN", 0, W + L), v("L4", 24, 36)), v("VY"))
        yield

    def sending(t):
        ms, hg = "ms%d" % t, "HGS%d" % t
        scan(v("CS"), v("k0", 256, 268), v("ZER", 0, 12), add, add)
        tt(v("DA"), v("CS"), v("k0", 272, 284), add)
        tt(v("DB"), v("DA"), v("TRL"), sub)
        tt(v("DA"), v("DB"), v("LOF"), mul)
        tt(v("DB"), v("DA"), v("TRL"), add)
        tc(v("LO16"), v("DB"))
        tc(at(v(hg), v("LO16")), v("HG"))
        tc(at(v(ms), v("LO16")), v("XL"))
        r = narrow(v(hg, 0, S), S, "RT", "RTS")
        tc(v("HI4"), r)
        ts(v("HI4B"), v("HI4"), 11, OP.logical_shift_right)
        tc(v(ms, S, SW_), v("HI4B"))
        ship("s", t, v(ms, 0, SW_))
        ts(v("HI4B"), v("HI4"), 2047, OP.bitwise_and)
        tc(v("HSW%d" % t), v("HI4B"))
        tc(v("HS%d" % t), v("HI4B"))
        yield

    def change_rest(t):
        tt(v("XG"), at(v("X"), v("SL")), v("XL"), add)
        ts(v("XG"), v("XG"), 0.5, sub, 0.5, mul)
        tc(v("XI"), v("XG"))
        tc(at(v("X", 0, W + L), v("L4", 12, 24)), v("XI"))
        tc(at(v("F2"), v("L4", 12, 24)), v("H"))
        tc(at(v("F1"), v("L4", 36, 48)), v("H"))
        yield

    def guests(t):
        if t >= 1:
            lr, a = "lr%d" % t, 1760 + S * (t - 1)
            tt(v("X", a, a + S), v(lr), v("FD"), mul)
            tt(v("F1", a, a + S), v("HROW%d" % (t - 1)), v("FD"), mul)
            tt(v("F2", a, a + S), v("HROW%d" % (t - 1)), v("FD"), mul)
            if t < 3:
                tc(v("GH", a, a + S), v("GHN%d" % (t - 1)))
        yield

    def note_sent(t):
        hg = "HGS%d" % t
        tc(v("HIR"), v(hg, 0, S))
        ts(v("HIR2"), v("HIR"), 2047, OP.bitwise_and)
        tc(v("HROW%d" % t), v("HIR2"))
        tt(v("RV"), v(hg, 0, S), v("HROW%d" % t), sub)
        ts(v("RV2"), v("RV"), 2048.0 + S * t, add)
        tt(v("GHN%d" % t), v("RV2"), v("COLC"), add)
        yield

    def returns(t):
        lr, a = "lr%d" % t, 1760 + S * (t - 1)
        hw, hs = "HSW%d" % (t - 1), "HS%d" % (t - 1)
        ts(v("FD"), v(lr), 256.0, lt)
        if t < 3:
            r = narrow(v("FD"), S, "RTB", "RTSB")
            tt(v("RZ"), v(hw), v("TR4", 0, 4), sub)
            tc(v("RVB"), at(v("SN", 0, W), v(hs)))
            tt(v("FDW"), v("RZ"), r, mul)
            ts(v("RV2B"), v("RVB"), v("MTC", 4 + t, 5 + t), mul)
            tt(v("RZ"), v("FDW"), v("TR4", 0, 4), add)
            ts(v("RTB"), v("COLC"), float(S * (t - 1)), add, v("MTC", t, t + 1), mul)
            tc(v("RL16"), v("RZ"))
            tt(v("RVB"), v("RV2B"), v("RTB"), add)
            ts(v("SN", a, a + S), v(lr), 256.0, lt, float(M), mul)
            tc(at(v("SN", 0, W + L), v("RL16")), v("RVB"))
        yield

    for kind, t in MSGS:
        k = "%s%d" % (kind, t)
        wr["l" + k] = [(0, 1 << 20, "remote", "a" + k, NENG)]
        total["a" + k] = NENG
    st = {"late": (3, [], record(constants_late()))}
    for t in range(T_):
        p, last = "%d" % t, "%d" % (t - 1)
        st["lanes1" + p] = (1, ["returns" + last] if t else [], record(lanes1(t)))
        st["lanes2" + p] = (1, ["lanes1" + p] + (["rest" + last, "guests" + last, "sending" + last] if t else ["late"]), record(lanes2(t)))
        if t:
            st["arrivals" + p] = (2, ["rest" + last, "guests" + last, "returns" + last], record(arrivals(t)))
        else:
            st["last"] = (6, ["lanes2" + p], record(constants_last()))
        st["own0" + p] = (2, ["lanes2" + p], record(own(0)))
        st["own1" + p] = (3, ["lanes2" + p], record(own(1)))
        st["own2" + p] = (4, ["lanes2" + p], record(own(2)))
        st["flags" + p] = (4, ["lanes2" + p, "last"], record(own_flags(t)))
        st["found" + p] = (1, ["own0" + p, "own1" + p, "own2" + p, "flags" + p], record(found(t)))
        st["adopt" + p] = (1, ["found" + p], record(adopt(t)))
        over = ["adopt" + p] + (["arrivals" + p] if t else [])
        if t < 3:
            st["slots" + p] = (2, ["found" + p] + (["arrivals" + p] if t else []), record(slots(t)))
            st["sending" + p] = (0, ["found" + p], record(sending(t)))
            st["sons" + p] = (1, over + ["slots" + p], record(change_sons(t)))
            st["noted" + p] = (5, ["sending" + p], record(note_sent(t)))
        st["returns" + p] = (4, (["sons" + p] if t < 3 else over) + (["noted" + last] if t else []), record(returns(t)) if t else [])
        st["rest" + p] = (4, over, record(change_rest(t)))
        st["guests" + p] = (4, ["rest" + p, "returns" + p], record(guests(t)))
    merge(st)

    fill(v("F1", M, 1760), 0.0)
    fill(v("F2", M, 1760), 0.0)
    fill(v("X", M, 1760), 0.0)
    dma("s", ("fo", 0, W, T.fo[:]), v("F1", 0, W, p=(0, 128, 16)))
    dma("y", ("xo", 0, W, T.xo[:]), v("X", 0, W))
    dma("s", ("f2o", 0, W, T.f2o[:]), v("F2", 0, W, p=(0, 128, 16)))
    for sem in sorted(total):
        g.wait_ge(T.sem[sem], total[sem])
    g.wait_ge(T.sem.lo, sent[0])
